import numpy as np
import ml_dtypes


def mxq(x, axis, fmt="e4m3"):
    dtype, down = {"e4m3": (ml_dtypes.float8_e4m3fn, 7), "e5m2": (ml_dtypes.float8_e5m2, 14)}[fmt]
    v = np.moveaxis(np.asarray(x, np.float32).astype(ml_dtypes.bfloat16).astype(np.float64), axis, -1)
    blocks = v.reshape(v.shape[:-1] + (-1, 32))
    amax = np.abs(blocks).max(-1, keepdims=True)
    byte = np.maximum(np.where(amax > 0, np.frexp(amax)[1] - 1 + 127, 0) - down, 1)
    scale = np.exp2(byte - 127.0)
    codes = (blocks / scale).astype(np.float32).astype(dtype).astype(np.float64)
    return np.moveaxis((codes * scale).reshape(v.shape), -1, axis)


WIDE = False


def mx_kscale(k):
    if not WIDE:
        return np.ones(k)
    levels = np.array([10, -10, 5, -5, 0])
    if k % 512:
        return np.exp2(np.random.permutation(np.resize(levels, k // 32))).repeat(32)
    a = np.empty((k // 512, 16))
    for p in range(k // 512):
        a[p, :8] = np.random.permutation(np.resize(levels, 8))
        for g in range(8):
            far = levels[np.abs(levels - a[p, g]) >= 10]
            a[p, g + 8] = far[np.random.randint(len(far))]
    return np.exp2(a.ravel()).repeat(32)


def f64(x):
    return np.asarray(x).astype(np.float64)


def striped(idx):
    return np.tile(idx.reshape(-1, 16).T, (8, 1)).astype(np.uint16)


def unstriped(offs):
    return offs[:16].T.reshape(-1).astype(np.int64)


E2M1 = np.array([0.0, 0.5, 1.0, 1.5, 2.0, 3.0, 4.0, 6.0, -0.0, -0.5, -1.0, -1.5, -2.0, -3.0, -4.0, -6.0])


def pack_weight(w, fmt):
    k, n = w.shape
    w = f64(np.asarray(w, np.float32).astype(ml_dtypes.bfloat16)).reshape(k // 32, 32, n)
    amax = np.abs(w).max(1)
    if fmt == "e4m3":
        byte = np.frexp(amax)[1] - 1 + 127 - 7
    else:
        mant, ex = np.frexp(amax / 6.0)
        byte = np.where(mant > 0.5, ex, ex - 1) + 127
    byte = np.clip(np.where(amax > 0, byte, 1), 1, 254)
    scaled = (w * np.exp2(127.0 - byte)[:, None, :]).reshape(k, n).astype(np.float32)
    by_word = np.ascontiguousarray(scaled.reshape(k // 512, 128, 4, n).transpose(0, 1, 3, 2))
    if fmt == "e4m3":
        words = by_word.astype(ml_dtypes.float8_e4m3fn).view(np.uint8)
    else:
        c = by_word.astype(ml_dtypes.float4_e2m1fn).view(np.uint8) & 0xF
        words = (c[..., 0::2] | (c[..., 1::2] << 4)).reshape(k // 512, 128, 2 * n)
    return np.ascontiguousarray(words), np.ascontiguousarray(byte.astype(np.uint8).reshape(k // 512, 16, n))


def unpack_weight(words, scales, fmt):
    g, _, n = scales.shape
    words = np.ascontiguousarray(words).reshape(g, 128, n, -1)
    if fmt == "e4m3":
        vals = words.view(ml_dtypes.float8_e4m3fn).astype(np.float64)
    else:
        nib = np.empty((g, 128, n, 4), np.uint8)
        nib[..., 0::2] = words & 0xF
        nib[..., 1::2] = words >> 4
        vals = E2M1[nib]
    vals = vals * np.repeat(np.exp2(scales.astype(np.float64) - 127.0), 8, axis=1)[..., None]
    return vals.transpose(0, 1, 3, 2).reshape(g * 512, n)


def relu(v):
    return np.maximum(v, 0.0)


K, L, T, Q, E, C, D = 512, 1024, 512, 1024, 4, 128, 128
H, N = 512, 512


def by_expert(wq, xq, C):
    return np.concatenate([wq[e].T @ xq[:, e * C:(e + 1) * C] for e in range(E)], axis=1)


def setup_inputs():
    n = np.random.standard_normal
    s = mx_kscale(K)
    v = mx_kscale(L)
    u = mx_kscale(H)
    slots1, slots2 = np.random.permutation(T)[:E * C], np.random.permutation(Q)[:E * D]
    x = pack_weight(n((K, T)) * s[:, None], "e4m3")
    z = pack_weight(n((L, Q)) * v[:, None], "e4m3")
    w1 = [pack_weight(m, "e4m3") for m in n((E, K, H)) / np.sqrt(K) / s[None, :, None] * u]
    w2 = [pack_weight(m, "e4m3") for m in n((E, H, N)) / np.sqrt(H) / u[None, :, None]]
    return {
        "x_words": x[0],
        "x_scales": x[1],
        "z_words": z[0],
        "z_scales": z[1],
        "w1_words": np.stack([m[0] for m in w1]),
        "w1_scales": np.stack([m[1] for m in w1]),
        "wz": (n((E, L, H)) / np.sqrt(L) / v[None, :, None] * u).astype(np.float32),
        "w2_words": np.stack([m[0] for m in w2]),
        "w2_scales": np.stack([m[1] for m in w2]),
        "gate1": (np.tile(np.random.uniform(0.2, 1.0, E * C), (128, 1))).astype(np.float32),
        "gate2": (np.tile(np.random.uniform(0.2, 1.0, E * D), (128, 1))).astype(np.float32),
        "offs": striped(slots1),
        "offs2": striped(slots2),
    }


def reference(x_words, x_scales, z_words, z_scales, w1_words, w1_scales, wz, w2_words, w2_scales, gate1, gate2, offs, offs2):
    w1 = np.stack([unpack_weight(w1_words[e], w1_scales[e], "e4m3") for e in range(E)])
    wzq = mxq(f64(wz), 1, "e4m3")
    w2 = np.stack([unpack_weight(w2_words[e], w2_scales[e], "e4m3") for e in range(E)])
    idx, idx2 = unstriped(offs), unstriped(offs2)
    xq = unpack_weight(x_words, x_scales, "e4m3")[:, idx]
    zq = unpack_weight(z_words, z_scales, "e4m3")[:, idx2]
    h = relu(by_expert(w1, xq, C))
    p = relu(by_expert(wzq, zq, D))
    out = np.zeros((N, T + Q))
    out[:, idx] = f64(gate1[:1]) * by_expert(w2, mxq(h, 0, "e4m3"), C)
    out[:, T + idx2] = f64(gate2[:1]) * by_expert(w2, mxq(p, 0, "e4m3"), D)
    return out

@@ -1,0 +1,240 @@
+from contextlib import ExitStack
+
+import concourse.mybir as mybir
+from concourse.masks import make_identity
+
+K, L, T, Q, E, C = 512, 1024, 512, 1024, 4, 128
+H, N = 512, 512
+FLOPS = 2 * E * C * (K * H + L * H + 2 * H * N)
+
+F32 = mybir.dt.float32
+BF16 = mybir.dt.bfloat16
+I32 = mybir.dt.int32
+U32 = mybir.dt.uint32
+U16 = mybir.dt.uint16
+U8 = mybir.dt.uint8
+FP8X4 = mybir.dt.float8_e4m3fn_x4
+RELU = mybir.ActivationFunctionType.Relu
+MULT = mybir.AluOpType.mult
+
+P = 128
+PACK = 4
+QUADS = 4
+Z_PASSES = L // (P * PACK)
+N_TILES = N // P
+COLS = C // 16
+
+
+def tile_moe_mmo_relu_kernel(
+    tc, x_words, x_scales, z_words, z_scales, w1_words, w1_scales, wz, w2_words, w2_scales,
+    gate1, gate2, offs, offs2, out
+):
+    nc = tc.nc
+    with ExitStack() as ctx:
+        keep = ctx.enter_context(tc.tile_pool(name="keep", bufs=1))
+        first = ctx.enter_context(tc.psum_pool(name="first", bufs=2))
+        turned = ctx.enter_context(tc.psum_pool(name="turned", bufs=1))
+        second = ctx.enter_context(tc.psum_pool(name="second", bufs=5))
+        shared = ctx.enter_context(tc.tile_pool(name="shared", bufs=1))
+
+        def held(shape, dtype, name):
+            return keep.tile(shape, dtype, name=name, align_bytes=64)
+
+        def reused(shape, dtype, name, slot):
+            return shared.tile(shape, dtype, name=name, tag=slot, align_bytes=64)
+
+        offs_t = held([P, E * COLS], U16, "offs_t")
+        offs2_t = held([P, E * COLS], U16, "offs2_t")
+        xw = held([P, T], I32, "xw")
+        xs = held([P, T], U8, "xs")
+        zw = [held([P, Q], I32, "zw%d" % s) for s in range(Z_PASSES)]
+        zs = held([P, Q], U8, "zs")
+        w1w = [held([P, 2, H], I32, "w1w%d" % a) for a in range(2)]
+        w2w = [held([P, 2, N], I32, "w2w%d" % a) for a in range(2)]
+        w1s = held([P, H], U8, "w1s")
+        w2s = held([P, N], U8, "w2s")
+        g1 = held([P, E * C], F32, "g1")
+        g2 = held([P, E * C], F32, "g2")
+        raw = [[held([P, PACK, H], F32, "raw%d%d" % (e, s)) for s in range(Z_PASSES)] for e in range(E)]
+        text_out = [held([P, T], F32, "text_out%d" % b) for b in range(N_TILES)]
+        patch_out = [held([P, Q], F32, "patch_out%d" % b) for b in range(N_TILES)]
+        ident = held([P, P], F32, "ident")
+
+        for plane in (xs, w1s, w2s, zs):
+            nc.vector.memset(plane[:].bitcast(I32), 0)
+        for b in range(2):
+            nc.vector.memset(patch_out[b][:], 0.0)
+        for b in range(2, N_TILES):
+            nc.scalar.activation(patch_out[b][:], patch_out[0][:], RELU)
+
+        def load_scales(queue, plane, rows):
+            count = rows.shape[0]
+            for q in range(QUADS):
+                queue.dma_start(
+                    out=plane[32 * q : 32 * q + 4 * count, :].bitcast(I32),
+                    in_=rows[:, 4 * q : 4 * q + 4, :].bitcast(I32),
+                )
+
+        def load_words(tile, words):
+            nc.sync.dma_start(out=tile[:], in_=words.rearrange("p c d -> p (c d)").bitcast(I32))
+
+        def load_pair(tile, words, a):
+            nc.sync.dma_start(
+                out=tile[:], in_=words[2 * a : 2 * a + 2, 0].rearrange("e p c d -> p e (c d)").bitcast(I32)
+            )
+
+        def load_wz(e, s):
+            rows = wz[e, s * P * PACK : (s + 1) * P * PACK, :]
+            nc.sync.dma_start(out=raw[e][s][:], in_=rows.rearrange("(p j) c -> p j c", j=PACK))
+
+        make_identity(nc, ident[:])
+        nc.sync.dma_start(offs_t[:], offs)
+        load_words(xw, x_words[0])
+        load_scales(nc.sync, xs, x_scales)
+        load_pair(w1w[0], w1_words, 0)
+        load_wz(0, 0)
+        load_scales(nc.sync, w1s, w1_scales[:, 0])
+        load_pair(w2w[0], w2_words, 0)
+        nc.sync.dma_start(out=g1[:], in_=gate1)
+        load_scales(nc.sync, w2s, w2_scales[:, 0])
+        load_wz(0, 1)
+        nc.sync.dma_start(offs2_t[:], offs2)
+        for s in range(Z_PASSES):
+            load_words(zw[s], z_words[s])
+        load_scales(nc.sync, zs, z_scales)
+        load_wz(1, 0)
+        load_pair(w1w[1], w1_words, 1)
+        load_pair(w2w[1], w2_words, 1)
+        load_wz(1, 1)
+        nc.sync.dma_start(out=g2[:], in_=gate2)
+        for e in (2, 3):
+            for s in range(Z_PASSES):
+                load_wz(e, s)
+
+        xg = held([P, E * C], U32, "xg")
+        xgs = held([P, E * C], U8, "xgs")
+        zg = [held([P, E * C], U32, "zg%d" % s) for s in range(Z_PASSES)]
+        zgs = held([P, E * C], U8, "zgs")
+
+        def gather_text(a):
+            slots = slice(2 * a * C, 2 * (a + 1) * C)
+            cols = offs_t[:, 2 * a * COLS : 2 * (a + 1) * COLS]
+            nc.vector.tensor_copy(xg[:, slots], xw[:].bitcast(U32).indirect(cols))
+            nc.vector.tensor_copy(xgs[:, slots], xs[:].indirect(cols))
+
+        def gather_patches():
+            for s in range(Z_PASSES):
+                nc.vector.tensor_copy(zg[s][:], zw[s][:].bitcast(U32).indirect(offs2_t[:]))
+            nc.vector.tensor_copy(zgs[:], zs[:].indirect(offs2_t[:]))
+
+        def text_hidden(e):
+            slots = slice(e * C, (e + 1) * C)
+            acc = first.tile([P, H], F32, name="acc1")
+            nc.tensor.matmul_mx(
+                out=acc[:], lhsT=xg[:, slots].bitcast(FP8X4), lhsT_scale=xgs[:, slots],
+                rhs=w1w[e // 2][:, e % 2, :].bitcast(FP8X4), rhs_scale=w1s[4 * e :, :], start=True, stop=True,
+            )
+            rows = held([P, H], BF16, "rows%d" % e)
+            nc.scalar.activation(rows[:], acc[:], RELU)
+            pairs = rows[:].bitcast(F32)
+            turn = turned.tile([P, 2, C], F32, name="turn")
+            for u in range(2):
+                nc.tensor.transpose(turn[:, u, :], pairs[:, u : H // 2 : 2], ident[:])
+            hidden = held([P, C, PACK], BF16, "hidden_t%d" % e)
+            nc.scalar.copy(
+                hidden[:].rearrange("p c t -> p (c t)").bitcast(F32).rearrange("p (c u) -> p c u", u=2),
+                turn[:].rearrange("p u c -> p c u"),
+            )
+            return hidden
+
+        def patch_hidden(e, quantised):
+            slots = slice(e * C, (e + 1) * C)
+            acc = first.tile([P, H], F32, name="acc1")
+            for t in range(PACK):
+                cols = slice(t * P, (t + 1) * P)
+                for s, (w, ws) in enumerate(quantised):
+                    nc.tensor.matmul_mx(
+                        out=acc[:, cols], lhsT=w[:, cols].bitcast(FP8X4), lhsT_scale=ws[:, cols],
+                        rhs=zg[s][:, slots].bitcast(FP8X4), rhs_scale=zgs[4 * s :, slots],
+                        start=(s == 0), stop=(s == Z_PASSES - 1),
+                    )
+            hidden = reused([P, C, PACK], BF16, "hidden_p%d" % e, "hidden_p%d" % e)
+            nc.scalar.activation(hidden[:], acc[:].rearrange("p (t c) -> p c t", t=PACK), RELU)
+            return hidden
+
+        def second_product(hidden, e, name):
+            codes = held([P, C], U32, "hcodes" + name)
+            scales = held([P, C], U8, "hscales" + name)
+            nc.vector.quantize_mx(
+                out=codes[:].bitcast(FP8X4), scales=scales[:], in_=hidden[:].rearrange("p c t -> p (c t)")
+            )
+            acc = second.tile([P, N_TILES, C], F32, name="acc2")
+            for b in range(N_TILES):
+                cols = slice(b * P, (b + 1) * P)
+                nc.tensor.matmul_mx(
+                    out=acc[:, b, :], lhsT=w2w[e // 2][:, e % 2, cols].bitcast(FP8X4),
+                    lhsT_scale=w2s[4 * e :, cols], rhs=codes[:].bitcast(FP8X4), rhs_scale=scales[:],
+                    start=True, stop=True,
+                )
+            return acc
+
+        def put_back(acc, gate, windows, offsets, e, name, slot):
+            res = reused([P, N_TILES, C], F32, "res" + name, slot)
+            g = gate[:, e * C : (e + 1) * C].unsqueeze(1).to_broadcast([P, N_TILES, C])
+            nc.vector.tensor_tensor(res[:], acc[:], g, MULT)
+            for b in range(N_TILES):
+                nc.vector.tensor_copy(
+                    windows[b][:].indirect(offsets[:, e * COLS : (e + 1) * COLS]), res[:, b, :]
+                )
+
+        def quantise_wz(e, s):
+            grouped = reused([P, PACK, P, PACK], BF16, "grouped%d%d" % (e, s), "grouped%d%d" % (e, s))
+            for half in range(2):
+                m = slice(half * P // 2, (half + 1) * P // 2)
+                nc.scalar.copy(
+                    grouped[:].rearrange("p t m j -> p m j t")[:, m],
+                    raw[e][s][:].rearrange("p j (m t) -> p m j t", t=PACK)[:, m],
+                )
+            codes = held([P, H], U32, "wcodes%d%d" % (e, s))
+            scales = held([P, H], U8, "wscales%d%d" % (e, s))
+            nc.vector.quantize_mx(
+                out=codes[:].bitcast(FP8X4), scales=scales[:], in_=grouped[:].rearrange("p t m j -> p (t m j)")
+            )
+            return codes, scales
+
+        def text_sums(e):
+            return second_product(text_hidden(e), e, "t%d" % e)
+
+        def patch_sums(e):
+            quantised = [quantise_wz(e, s) for s in range(Z_PASSES)]
+            return second_product(patch_hidden(e, quantised), e, "p%d" % e)
+
+        def put_text(acc, e, slot):
+            put_back(acc, g1, text_out, offs_t, e, "t%d" % e, slot)
+
+        def put_patches(acc, e, slot):
+            put_back(acc, g2, patch_out, offs2_t, e, "p%d" % e, slot)
+
+        gather_text(0)
+        t0 = text_sums(0)
+        t1 = text_sums(1)
+        gather_text(1)
+        gather_patches()
+        put_text(t0, 0, "own_t0")
+        p0 = patch_sums(0)
+        put_text(t1, 1, "grouped01")
+        t2 = text_sums(2)
+        t3 = text_sums(3)
+        p1 = patch_sums(1)
+        put_text(t2, 2, "grouped11")
+        put_patches(p0, 0, "hidden_p1")
+        p2 = patch_sums(2)
+        put_text(t3, 3, "grouped21")
+        put_patches(p1, 1, "hidden_p2")
+        p3 = patch_sums(3)
+        put_patches(p2, 2, "grouped31")
+        put_patches(p3, 3, "own_p3")
+        for b in range(N_TILES):
+            nc.sync.dma_start(out=out[b * P : (b + 1) * P, 0:T], in_=text_out[b][:])
+        for b in range(N_TILES):
+            nc.sync.dma_start(out=out[b * P : (b + 1) * P, T : T + Q], in_=patch_out[b][:])

@@ -23,6 +23,8 @@ QUADS = 4
 Z_PASSES = L // (P * PACK)
 N_TILES = N // P
 COLS = C // 16
+RAW_BYTES = PACK * H * 4
+PART_BYTES = 2048
 
 
 def tile_moe_mmo_relu_kernel(
@@ -33,15 +35,24 @@ def tile_moe_mmo_relu_kernel(
     with ExitStack() as ctx:
         keep = ctx.enter_context(tc.tile_pool(name="keep", bufs=1))
         first = ctx.enter_context(tc.psum_pool(name="first", bufs=2))
-        turned = ctx.enter_context(tc.psum_pool(name="turned", bufs=1))
-        second = ctx.enter_context(tc.psum_pool(name="second", bufs=5))
+        turned = ctx.enter_context(tc.psum_pool(name="turned", bufs=2))
+        second = ctx.enter_context(tc.psum_pool(name="second", bufs=4))
         shared = ctx.enter_context(tc.tile_pool(name="shared", bufs=1))
 
         def held(shape, dtype, name):
             return keep.tile(shape, dtype, name=name, align_bytes=64)
 
-        def reused(shape, dtype, name, slot):
-            return shared.tile(shape, dtype, name=name, tag=slot, align_bytes=64)
+        def placed(shape, dtype, name, offset):
+            return shared.tile(shape, dtype, name=name, offset=offset, align_bytes=64)
+
+        def place(shape, dtype, name, offset):
+            return held(shape, dtype, name) if offset is None else placed(shape, dtype, name, offset)
+
+        def raw_at(e, s, part=0):
+            return (Z_PASSES * e + s) * RAW_BYTES + part * PART_BYTES
+
+        rows_at = E * Z_PASSES * RAW_BYTES + 512
+        codes_at = rows_at + PART_BYTES - 512
 
         offs_t = held([P, E * COLS], U16, "offs_t")
         offs2_t = held([P, E * COLS], U16, "offs2_t")
@@ -55,7 +66,7 @@ def tile_moe_mmo_relu_kernel(
         w2s = held([P, N], U8, "w2s")
         g1 = held([P, E * C], F32, "g1")
         g2 = held([P, E * C], F32, "g2")
-        raw = [[held([P, PACK, H], F32, "raw%d%d" % (e, s)) for s in range(Z_PASSES)] for e in range(E)]
+        raw = [[placed([P, PACK, H], F32, "raw%d%d" % (e, s), raw_at(e, s)) for s in range(Z_PASSES)] for e in range(E)]
         text_out = [held([P, T], F32, "text_out%d" % b) for b in range(N_TILES)]
         patch_out = [held([P, Q], F32, "patch_out%d" % b) for b in range(N_TILES)]
         ident = held([P, P], F32, "ident")
@@ -90,23 +101,23 @@ def tile_moe_mmo_relu_kernel(
         make_identity(nc, ident[:])
         nc.sync.dma_start(offs_t[:], offs)
         load_words(xw, x_words[0])
-        load_scales(nc.sync, xs, x_scales)
-        load_pair(w1w[0], w1_words, 0)
-        load_wz(0, 0)
-        load_scales(nc.sync, w1s, w1_scales[:, 0])
-        load_pair(w2w[0], w2_words, 0)
-        nc.sync.dma_start(out=g1[:], in_=gate1)
-        load_scales(nc.sync, w2s, w2_scales[:, 0])
-        load_wz(0, 1)
         nc.sync.dma_start(offs2_t[:], offs2)
-        for s in range(Z_PASSES):
-            load_words(zw[s], z_words[s])
+        load_scales(nc.sync, xs, x_scales)
+        load_words(zw[0], z_words[0])
+        load_pair(w1w[0], w1_words, 0)
+        load_scales(nc.sync, w1s, w1_scales[:, 0])
+        load_words(zw[1], z_words[1])
         load_scales(nc.sync, zs, z_scales)
-        load_wz(1, 0)
+        load_pair(w2w[0], w2_words, 0)
+        load_scales(nc.sync, w2s, w2_scales[:, 0])
+        nc.sync.dma_start(out=g1[:], in_=gate1)
         load_pair(w1w[1], w1_words, 1)
+        load_wz(0, 0)
         load_pair(w2w[1], w2_words, 1)
-        load_wz(1, 1)
+        load_wz(0, 1)
+        load_wz(1, 0)
         nc.sync.dma_start(out=g2[:], in_=gate2)
+        load_wz(1, 1)
         for e in (2, 3):
             for s in range(Z_PASSES):
                 load_wz(e, s)
@@ -134,7 +145,7 @@ def tile_moe_mmo_relu_kernel(
                 out=acc[:], lhsT=xg[:, slots].bitcast(FP8X4), lhsT_scale=xgs[:, slots],
                 rhs=w1w[e // 2][:, e % 2, :].bitcast(FP8X4), rhs_scale=w1s[4 * e :, :], start=True, stop=True,
             )
-            rows = held([P, H], BF16, "rows%d" % e)
+            rows = place([P, H], BF16, "rows%d" % e, rows_at if e == E - 1 else None)
             nc.scalar.activation(rows[:], acc[:], RELU)
             pairs = rows[:].bitcast(F32)
             turn = turned.tile([P, 2, C], F32, name="turn")
@@ -147,7 +158,7 @@ def tile_moe_mmo_relu_kernel(
             )
             return hidden
 
-        def patch_hidden(e, quantised):
+        def patch_hidden(e, quantised, offset):
             slots = slice(e * C, (e + 1) * C)
             acc = first.tile([P, H], F32, name="acc1")
             for t in range(PACK):
@@ -158,7 +169,7 @@ def tile_moe_mmo_relu_kernel(
                         rhs=zg[s][:, slots].bitcast(FP8X4), rhs_scale=zgs[4 * s :, slots],
                         start=(s == 0), stop=(s == Z_PASSES - 1),
                     )
-            hidden = reused([P, C, PACK], BF16, "hidden_p%d" % e, "hidden_p%d" % e)
+            hidden = place([P, C, PACK], BF16, "hidden_p%d" % e, offset)
             nc.scalar.activation(hidden[:], acc[:].rearrange("p (t c) -> p c t", t=PACK), RELU)
             return hidden
 
@@ -178,24 +189,23 @@ def tile_moe_mmo_relu_kernel(
                 )
             return acc
 
-        def put_back(acc, gate, windows, offsets, e, name, slot):
-            res = reused([P, N_TILES, C], F32, "res" + name, slot)
-            g = gate[:, e * C : (e + 1) * C].unsqueeze(1).to_broadcast([P, N_TILES, C])
-            nc.vector.tensor_tensor(res[:], acc[:], g, MULT)
-            for b in range(N_TILES):
-                nc.vector.tensor_copy(
-                    windows[b][:].indirect(offsets[:, e * COLS : (e + 1) * COLS]), res[:, b, :]
+        def put_back(acc, gate, windows, offsets, e, half, name, offset):
+            res = place([P, 2, C], F32, "res%s%d" % (name, half), offset)
+            nc.scalar.copy(res[:], acc[:, 2 * half : 2 * half + 2, :])
+            for b in range(2):
+                nc.vector.tensor_tensor(
+                    windows[2 * half + b][:].indirect(offsets[:, e * COLS : (e + 1) * COLS]),
+                    res[:, b, :], gate[:, e * C : (e + 1) * C], MULT,
                 )
 
         def quantise_wz(e, s):
-            grouped = reused([P, PACK, P, PACK], BF16, "grouped%d%d" % (e, s), "grouped%d%d" % (e, s))
-            for half in range(2):
-                m = slice(half * P // 2, (half + 1) * P // 2)
-                nc.scalar.copy(
-                    grouped[:].rearrange("p t m j -> p m j t")[:, m],
-                    raw[e][s][:].rearrange("p j (m t) -> p m j t", t=PACK)[:, m],
-                )
-            codes = held([P, H], U32, "wcodes%d%d" % (e, s))
+            grouped = held([P, PACK, P, PACK], BF16, "grouped%d%d" % (e, s))
+            nc.scalar.copy(
+                grouped[:].rearrange("p t m j -> p m j t"),
+                raw[e][s][:].rearrange("p j (m t) -> p m j t", t=PACK),
+            )
+            last = (e, s) == (E - 1, Z_PASSES - 1)
+            codes = place([P, H], U32, "wcodes%d%d" % (e, s), codes_at if last else None)
             scales = held([P, H], U8, "wscales%d%d" % (e, s))
             nc.vector.quantize_mx(
                 out=codes[:].bitcast(FP8X4), scales=scales[:], in_=grouped[:].rearrange("p t m j -> p (t m j)")
@@ -205,35 +215,49 @@ def tile_moe_mmo_relu_kernel(
         def text_sums(e):
             return second_product(text_hidden(e), e, "t%d" % e)
 
-        def patch_sums(e):
-            quantised = [quantise_wz(e, s) for s in range(Z_PASSES)]
-            return second_product(patch_hidden(e, quantised), e, "p%d" % e)
+        def patch_sums(e, quantised, offset):
+            return second_product(patch_hidden(e, quantised, offset), e, "p%d" % e)
 
-        def put_text(acc, e, slot):
-            put_back(acc, g1, text_out, offs_t, e, "t%d" % e, slot)
+        def put_text(acc, e, half, offset):
+            put_back(acc, g1, text_out, offs_t, e, half, "t%d" % e, offset)
 
-        def put_patches(acc, e, slot):
-            put_back(acc, g2, patch_out, offs2_t, e, "p%d" % e, slot)
+        def put_patches(acc, e, half, offset):
+            put_back(acc, g2, patch_out, offs2_t, e, half, "p%d" % e, offset)
 
         gather_text(0)
+        gather_text(1)
         t0 = text_sums(0)
         t1 = text_sums(1)
-        gather_text(1)
         gather_patches()
-        put_text(t0, 0, "own_t0")
-        p0 = patch_sums(0)
-        put_text(t1, 1, "grouped01")
+        put_text(t0, 0, 0, None)
+        put_text(t0, 0, 1, None)
         t2 = text_sums(2)
         t3 = text_sums(3)
-        p1 = patch_sums(1)
-        put_text(t2, 2, "grouped11")
-        put_patches(p0, 0, "hidden_p1")
-        p2 = patch_sums(2)
-        put_text(t3, 3, "grouped21")
-        put_patches(p1, 1, "hidden_p2")
-        p3 = patch_sums(3)
-        put_patches(p2, 2, "grouped31")
-        put_patches(p3, 3, "own_p3")
+        put_text(t1, 1, 0, rows_at - 512)
+        put_text(t1, 1, 1, rows_at + 512)
+        q0 = [quantise_wz(0, 0), quantise_wz(0, 1)]
+        put_text(t2, 2, 0, raw_at(0, 1, 0))
+        put_text(t2, 2, 1, raw_at(0, 1, 1))
+        q1 = [quantise_wz(1, 0)]
+        p0 = patch_sums(0, q0, raw_at(1, 0, 0))
+        put_text(t3, 3, 0, raw_at(1, 0, 1))
+        q1.append(quantise_wz(1, 1))
+        put_text(t3, 3, 1, raw_at(1, 1, 0))
+        put_patches(p0, 0, 0, raw_at(1, 1, 1))
+        q2 = [quantise_wz(2, 0)]
+        p1 = patch_sums(1, q1, raw_at(2, 0, 0))
+        put_patches(p0, 0, 1, raw_at(2, 0, 1))
+        q2.append(quantise_wz(2, 1))
+        put_patches(p1, 1, 0, raw_at(2, 1, 0))
+        q3 = [quantise_wz(3, 0)]
+        p2 = patch_sums(2, q2, raw_at(3, 0, 0))
+        put_patches(p1, 1, 1, raw_at(3, 0, 1))
+        q3.append(quantise_wz(3, 1))
+        put_patches(p2, 2, 0, raw_at(3, 1, 0))
+        p3 = patch_sums(3, q3, None)
+        put_patches(p2, 2, 1, codes_at)
+        put_patches(p3, 3, 0, None)
+        put_patches(p3, 3, 1, None)
         for b in range(N_TILES):
             nc.sync.dma_start(out=out[b * P : (b + 1) * P, 0:T], in_=text_out[b][:])
         for b in range(N_TILES):

@@ -23,6 +23,7 @@ QUADS = 4
 Z_PASSES = L // (P * PACK)
 N_TILES = N // P
 COLS = C // 16
+X_WINDOW = 768
 RAW_BYTES = PACK * H * 4
 PART_BYTES = 2048
 
@@ -51,13 +52,14 @@ def tile_moe_mmo_relu_kernel(
         def raw_at(e, s, part=0):
             return (Z_PASSES * e + s) * RAW_BYTES + part * PART_BYTES
 
-        rows_at = E * Z_PASSES * RAW_BYTES + 512
-        codes_at = rows_at + PART_BYTES - 512
+        rows_at = E * Z_PASSES * RAW_BYTES
+        hcodes_at = rows_at + 3 * PART_BYTES
+        codes_at = rows_at + 2 * PART_BYTES
 
         offs_t = held([P, E * COLS], U16, "offs_t")
         offs2_t = held([P, E * COLS], U16, "offs2_t")
-        xw = held([P, T], I32, "xw")
-        xs = held([P, T], U8, "xs")
+        xw = held([P, X_WINDOW], I32, "xw")
+        xs = held([P, X_WINDOW], U8, "xs")
         zw = [held([P, Q], I32, "zw%d" % s) for s in range(Z_PASSES)]
         zs = held([P, Q], U8, "zs")
         w1w = [held([P, 2, H], I32, "w1w%d" % a) for a in range(2)]
@@ -73,6 +75,7 @@ def tile_moe_mmo_relu_kernel(
 
         for plane in (xs, w1s, w2s, zs):
             nc.vector.memset(plane[:].bitcast(I32), 0)
+        nc.vector.memset(xw[:, T:], 0)
         for b in range(2):
             nc.vector.memset(patch_out[b][:], 0.0)
         for b in range(2, N_TILES):
@@ -82,12 +85,12 @@ def tile_moe_mmo_relu_kernel(
             count = rows.shape[0]
             for q in range(QUADS):
                 queue.dma_start(
-                    out=plane[32 * q : 32 * q + 4 * count, :].bitcast(I32),
+                    out=plane[32 * q : 32 * q + 4 * count, 0 : rows.shape[2]].bitcast(I32),
                     in_=rows[:, 4 * q : 4 * q + 4, :].bitcast(I32),
                 )
 
         def load_words(tile, words):
-            nc.sync.dma_start(out=tile[:], in_=words.rearrange("p c d -> p (c d)").bitcast(I32))
+            nc.sync.dma_start(out=tile[:, 0 : words.shape[1]], in_=words.rearrange("p c d -> p (c d)").bitcast(I32))
 
         def load_pair(tile, words, a):
             nc.sync.dma_start(
@@ -99,66 +102,62 @@ def tile_moe_mmo_relu_kernel(
             nc.sync.dma_start(out=raw[e][s][:], in_=rows.rearrange("(p j) c -> p j c", j=PACK))
 
         make_identity(nc, ident[:])
-        nc.sync.dma_start(offs_t[:], offs)
         load_words(xw, x_words[0])
-        nc.sync.dma_start(offs2_t[:], offs2)
+        nc.sync.dma_start(offs_t[:], offs)
         load_scales(nc.sync, xs, x_scales)
-        load_words(zw[0], z_words[0])
         load_pair(w1w[0], w1_words, 0)
+        load_words(zw[0], z_words[0])
         load_scales(nc.sync, w1s, w1_scales[:, 0])
+        nc.sync.dma_start(offs2_t[:], offs2)
         load_words(zw[1], z_words[1])
-        load_scales(nc.sync, zs, z_scales)
         load_pair(w2w[0], w2_words, 0)
-        load_scales(nc.sync, w2s, w2_scales[:, 0])
         nc.sync.dma_start(out=g1[:], in_=gate1)
+        load_scales(nc.sync, w2s, w2_scales[:, 0])
         load_pair(w1w[1], w1_words, 1)
-        load_wz(0, 0)
         load_pair(w2w[1], w2_words, 1)
-        load_wz(0, 1)
-        load_wz(1, 0)
-        nc.sync.dma_start(out=g2[:], in_=gate2)
-        load_wz(1, 1)
-        for e in (2, 3):
+        for e in range(2):
             for s in range(Z_PASSES):
                 load_wz(e, s)
+        load_scales(nc.sync, zs, z_scales)
+        load_wz(2, 0)
+        nc.sync.dma_start(out=g2[:], in_=gate2)
+        load_wz(2, 1)
+        load_wz(3, 0)
+        load_wz(3, 1)
 
         xg = held([P, E * C], U32, "xg")
         xgs = held([P, E * C], U8, "xgs")
         zg = [held([P, E * C], U32, "zg%d" % s) for s in range(Z_PASSES)]
         zgs = held([P, E * C], U8, "zgs")
 
-        def gather_text(a):
-            slots = slice(2 * a * C, 2 * (a + 1) * C)
-            cols = offs_t[:, 2 * a * COLS : 2 * (a + 1) * COLS]
-            nc.vector.tensor_copy(xg[:, slots], xw[:].bitcast(U32).indirect(cols))
-            nc.vector.tensor_copy(xgs[:, slots], xs[:].indirect(cols))
+        def gather_text():
+            nc.vector.tensor_copy(xg[:], xw[:].bitcast(U32).indirect(offs_t[:]))
+            nc.vector.tensor_copy(xgs[:], xs[:].indirect(offs_t[:]))
 
         def gather_patches():
             for s in range(Z_PASSES):
                 nc.vector.tensor_copy(zg[s][:], zw[s][:].bitcast(U32).indirect(offs2_t[:]))
             nc.vector.tensor_copy(zgs[:], zs[:].indirect(offs2_t[:]))
 
-        def text_hidden(e):
+        def text_hidden(e, hidden):
             slots = slice(e * C, (e + 1) * C)
             acc = first.tile([P, H], F32, name="acc1")
             nc.tensor.matmul_mx(
                 out=acc[:], lhsT=xg[:, slots].bitcast(FP8X4), lhsT_scale=xgs[:, slots],
                 rhs=w1w[e // 2][:, e % 2, :].bitcast(FP8X4), rhs_scale=w1s[4 * e :, :], start=True, stop=True,
             )
-            rows = place([P, H], BF16, "rows%d" % e, rows_at if e == E - 1 else None)
+            rows = place([P, H], BF16, "rows%d" % e, rows_at + 1024 if e == E - 1 else None)
             nc.scalar.activation(rows[:], acc[:], RELU)
             pairs = rows[:].bitcast(F32)
             turn = turned.tile([P, 2, C], F32, name="turn")
             for u in range(2):
                 nc.tensor.transpose(turn[:, u, :], pairs[:, u : H // 2 : 2], ident[:])
-            hidden = held([P, C, PACK], BF16, "hidden_t%d" % e)
             nc.scalar.copy(
-                hidden[:].rearrange("p c t -> p (c t)").bitcast(F32).rearrange("p (c u) -> p c u", u=2),
+                hidden.rearrange("p c t -> p (c t)").bitcast(F32).rearrange("p (c u) -> p c u", u=2),
                 turn[:].rearrange("p u c -> p c u"),
             )
-            return hidden
 
-        def patch_hidden(e, quantised, offset):
+        def patch_hidden(e, quantised, hidden):
             slots = slice(e * C, (e + 1) * C)
             acc = first.tile([P, H], F32, name="acc1")
             for t in range(PACK):
@@ -169,42 +168,53 @@ def tile_moe_mmo_relu_kernel(
                         rhs=zg[s][:, slots].bitcast(FP8X4), rhs_scale=zgs[4 * s :, slots],
                         start=(s == 0), stop=(s == Z_PASSES - 1),
                     )
-            hidden = place([P, C, PACK], BF16, "hidden_p%d" % e, offset)
-            nc.scalar.activation(hidden[:], acc[:].rearrange("p (t c) -> p c t", t=PACK), RELU)
-            return hidden
+            nc.scalar.activation(hidden, acc[:].rearrange("p (t c) -> p c t", t=PACK), RELU)
 
-        def second_product(hidden, e, name):
-            codes = held([P, C], U32, "hcodes" + name)
-            scales = held([P, C], U8, "hscales" + name)
+        def second_product(hidden, e0, count, name):
+            width = count * C
+            codes = place([P, width], U32, "hcodes" + name, hcodes_at if name == "p3" else None)
+            scales = held([P, width], U8, "hscales" + name)
             nc.vector.quantize_mx(
                 out=codes[:].bitcast(FP8X4), scales=scales[:], in_=hidden[:].rearrange("p c t -> p (c t)")
             )
-            acc = second.tile([P, N_TILES, C], F32, name="acc2")
-            for b in range(N_TILES):
-                cols = slice(b * P, (b + 1) * P)
-                nc.tensor.matmul_mx(
-                    out=acc[:, b, :], lhsT=w2w[e // 2][:, e % 2, cols].bitcast(FP8X4),
-                    lhsT_scale=w2s[4 * e :, cols], rhs=codes[:].bitcast(FP8X4), rhs_scale=scales[:],
-                    start=True, stop=True,
-                )
-            return acc
+            per_bank = N_TILES // count
+            halves = []
+            for bank in range(count):
+                acc = second.tile([P, per_bank, width], F32, name="acc2")
+                for i in range(count):
+                    e = e0 + i
+                    slots = slice(i * C, (i + 1) * C)
+                    for b in range(per_bank):
+                        cols = slice((bank * per_bank + b) * P, (bank * per_bank + b + 1) * P)
+                        nc.tensor.matmul_mx(
+                            out=acc[:, b, slots], lhsT=w2w[e // 2][:, e % 2, cols].bitcast(FP8X4),
+                            lhsT_scale=w2s[4 * e :, cols], rhs=codes[:, slots].bitcast(FP8X4),
+                            rhs_scale=scales[:, slots], start=True, stop=True,
+                        )
+                halves += [acc[:, b : b + 2, :] for b in range(0, per_bank, 2)]
+            return halves
 
-        def put_back(acc, gate, windows, offsets, e, half, name, offset):
-            res = place([P, 2, C], F32, "res%s%d" % (name, half), offset)
-            nc.scalar.copy(res[:], acc[:, 2 * half : 2 * half + 2, :])
+        def put_back(halves, gate, windows, offsets, e0, half, name, offset):
+            width = halves[half].shape[2]
+            res = place([P, 2, width], F32, "res%s%d" % (name, half), offset)
+            nc.scalar.copy(res[:], halves[half])
             for b in range(2):
                 nc.vector.tensor_tensor(
-                    windows[2 * half + b][:].indirect(offsets[:, e * COLS : (e + 1) * COLS]),
-                    res[:, b, :], gate[:, e * C : (e + 1) * C], MULT,
+                    windows[2 * half + b][:].indirect(offsets[:, e0 * COLS : e0 * COLS + width // 16]),
+                    res[:, b, :], gate[:, e0 * C : e0 * C + width], MULT,
                 )
 
-        def quantise_wz(e, s):
-            grouped = held([P, PACK, P, PACK], BF16, "grouped%d%d" % (e, s))
-            nc.scalar.copy(
-                grouped[:].rearrange("p t m j -> p m j t"),
-                raw[e][s][:].rearrange("p j (m t) -> p m j t", t=PACK),
-            )
+        def quantise_wz(e, s, offset=None):
+            shared_cast = offset is not None
+            grouped = place([P, PACK, P, PACK], BF16, "grouped%d%d" % (e, s), offset)
+            dst = grouped[:].rearrange("p t m j -> p m j t")
+            src = raw[e][s][:].rearrange("p j (m t) -> p m j t", t=PACK)
             last = (e, s) == (E - 1, Z_PASSES - 1)
+            if shared_cast:
+                nc.scalar.copy(dst[:, : P // 2], src[:, : P // 2])
+                nc.vector.tensor_copy(dst[:, P // 2 :], src[:, P // 2 :])
+            else:
+                nc.scalar.copy(dst, src)
             codes = place([P, H], U32, "wcodes%d%d" % (e, s), codes_at if last else None)
             scales = held([P, H], U8, "wscales%d%d" % (e, s))
             nc.vector.quantize_mx(
@@ -212,51 +222,47 @@ def tile_moe_mmo_relu_kernel(
             )
             return codes, scales
 
-        def text_sums(e):
-            return second_product(text_hidden(e), e, "t%d" % e)
+        def text_sums(e0):
+            hidden = held([P, 2 * C, PACK], BF16, "hidden_t%d" % e0)
+            for i in range(2):
+                text_hidden(e0 + i, hidden[:, i * C : (i + 1) * C, :])
+            return second_product(hidden, e0, 2, "t%d" % e0)
 
-        def patch_sums(e, quantised, offset):
-            return second_product(patch_hidden(e, quantised, offset), e, "p%d" % e)
+        def patch_sums(e0, quantised, offset):
+            hidden = place([P, len(quantised) * C, PACK], BF16, "hidden_p%d" % e0, offset)
+            for i, passes in enumerate(quantised):
+                patch_hidden(e0 + i, passes, hidden[:, i * C : (i + 1) * C, :])
+            return second_product(hidden, e0, len(quantised), "p%d" % e0)
 
-        def put_text(acc, e, half, offset):
-            put_back(acc, g1, text_out, offs_t, e, half, "t%d" % e, offset)
+        def put_text(halves, e0, half, offset):
+            put_back(halves, g1, text_out, offs_t, e0, half, "t%d" % e0, offset)
 
-        def put_patches(acc, e, half, offset):
-            put_back(acc, g2, patch_out, offs2_t, e, half, "p%d" % e, offset)
+        def put_patches(halves, e0, half, offset):
+            put_back(halves, g2, patch_out, offs2_t, e0, half, "p%d" % e0, offset)
 
-        gather_text(0)
-        gather_text(1)
-        t0 = text_sums(0)
-        t1 = text_sums(1)
+        gather_text()
         gather_patches()
-        put_text(t0, 0, 0, None)
-        put_text(t0, 0, 1, None)
-        t2 = text_sums(2)
-        t3 = text_sums(3)
-        put_text(t1, 1, 0, rows_at - 512)
-        put_text(t1, 1, 1, rows_at + 512)
-        q0 = [quantise_wz(0, 0), quantise_wz(0, 1)]
-        put_text(t2, 2, 0, raw_at(0, 1, 0))
-        put_text(t2, 2, 1, raw_at(0, 1, 1))
-        q1 = [quantise_wz(1, 0)]
-        p0 = patch_sums(0, q0, raw_at(1, 0, 0))
-        put_text(t3, 3, 0, raw_at(1, 0, 1))
-        q1.append(quantise_wz(1, 1))
-        put_text(t3, 3, 1, raw_at(1, 1, 0))
-        put_patches(p0, 0, 0, raw_at(1, 1, 1))
+        t01 = text_sums(0)
+        put_text(t01, 0, 0, None)
+        t23 = text_sums(2)
+        put_text(t01, 0, 1, rows_at + 1024)
+        q0 = [quantise_wz(0, 0)]
+        put_text(t23, 2, 0, raw_at(0, 0))
+        q0.append(quantise_wz(0, 1))
+        q1 = [quantise_wz(1, 0), quantise_wz(1, 1)]
+        put_text(t23, 2, 1, raw_at(1, 1))
         q2 = [quantise_wz(2, 0)]
-        p1 = patch_sums(1, q1, raw_at(2, 0, 0))
-        put_patches(p0, 0, 1, raw_at(2, 0, 1))
-        q2.append(quantise_wz(2, 1))
-        put_patches(p1, 1, 0, raw_at(2, 1, 0))
-        q3 = [quantise_wz(3, 0)]
-        p2 = patch_sums(2, q2, raw_at(3, 0, 0))
-        put_patches(p1, 1, 1, raw_at(3, 0, 1))
+        p01 = patch_sums(0, [q0, q1], raw_at(2, 0))
+        q2.append(quantise_wz(2, 1, raw_at(2, 0, 2)))
+        q3 = [quantise_wz(3, 0, raw_at(2, 1))]
+        put_patches(p01, 0, 0, raw_at(3, 0))
         q3.append(quantise_wz(3, 1))
-        put_patches(p2, 2, 0, raw_at(3, 1, 0))
-        p3 = patch_sums(3, q3, None)
-        put_patches(p2, 2, 1, codes_at)
+        p2 = patch_sums(2, [q2], raw_at(3, 1, 0))
+        put_patches(p01, 0, 1, raw_at(3, 1, 1))
+        p3 = patch_sums(3, [q3], None)
+        put_patches(p2, 2, 0, codes_at)
         put_patches(p3, 3, 0, None)
+        put_patches(p2, 2, 1, hcodes_at)
         put_patches(p3, 3, 1, None)
         for b in range(N_TILES):
             nc.sync.dma_start(out=out[b * P : (b + 1) * P, 0:T], in_=text_out[b][:])

@@ -23,7 +23,8 @@ QUADS = 4
 Z_PASSES = L // (P * PACK)
 N_TILES = N // P
 COLS = C // 16
-X_WINDOW = 768
+PASSES = E * Z_PASSES
+HALVED = (0, 1)
 RAW_BYTES = PACK * H * 4
 PART_BYTES = 2048
 
@@ -49,136 +50,132 @@ def tile_moe_mmo_relu_kernel(
         def place(shape, dtype, name, offset):
             return held(shape, dtype, name) if offset is None else placed(shape, dtype, name, offset)
 
-        def raw_at(e, s, part=0):
-            return (Z_PASSES * e + s) * RAW_BYTES + part * PART_BYTES
+        def raw_at(k, part=0):
+            return k * RAW_BYTES + part * PART_BYTES
 
-        rows_at = E * Z_PASSES * RAW_BYTES
-        hcodes_at = rows_at + 3 * PART_BYTES
-        codes_at = rows_at + 2 * PART_BYTES
+        codes_at = PASSES * RAW_BYTES
+        hcodes_at = codes_at + PART_BYTES
 
         offs_t = held([P, E * COLS], U16, "offs_t")
         offs2_t = held([P, E * COLS], U16, "offs2_t")
-        xw = held([P, X_WINDOW], I32, "xw")
-        xs = held([P, X_WINDOW], U8, "xs")
+        xw = held([P, T], I32, "xw")
+        xs = held([P, T], U8, "xs")
         zw = [held([P, Q], I32, "zw%d" % s) for s in range(Z_PASSES)]
         zs = held([P, Q], U8, "zs")
         w1w = [held([P, 2, H], I32, "w1w%d" % a) for a in range(2)]
         w2w = [held([P, 2, N], I32, "w2w%d" % a) for a in range(2)]
         w1s = held([P, H], U8, "w1s")
         w2s = held([P, N], U8, "w2s")
-        g1 = held([P, E * C], F32, "g1")
+        g1 = [held([P, 2 * C], F32, "g1%d" % a) for a in range(2)]
         g2 = held([P, E * C], F32, "g2")
-        raw = [[placed([P, PACK, H], F32, "raw%d%d" % (e, s), raw_at(e, s)) for s in range(Z_PASSES)] for e in range(E)]
+        raw = {}
+        for k in range(PASSES):
+            parts = 2 if k in HALVED else 1
+            for h in range(parts):
+                raw[k, h] = placed([P, PACK, H // parts], F32, "raw%d%d" % (k, h), raw_at(k, 2 * h))
         text_out = [held([P, T], F32, "text_out%d" % b) for b in range(N_TILES)]
         patch_out = [held([P, Q], F32, "patch_out%d" % b) for b in range(N_TILES)]
         ident = held([P, P], F32, "ident")
 
         for plane in (xs, w1s, w2s, zs):
             nc.vector.memset(plane[:].bitcast(I32), 0)
-        nc.vector.memset(xw[:, T:], 0)
         for b in range(2):
             nc.vector.memset(patch_out[b][:], 0.0)
         for b in range(2, N_TILES):
             nc.scalar.activation(patch_out[b][:], patch_out[0][:], RELU)
 
-        def load_scales(queue, plane, rows):
+        def load_scales(plane, rows, queue=nc.sync):
             count = rows.shape[0]
             for q in range(QUADS):
                 queue.dma_start(
-                    out=plane[32 * q : 32 * q + 4 * count, 0 : rows.shape[2]].bitcast(I32),
+                    out=plane[32 * q : 32 * q + 4 * count, :].bitcast(I32),
                     in_=rows[:, 4 * q : 4 * q + 4, :].bitcast(I32),
                 )
 
         def load_words(tile, words):
-            nc.sync.dma_start(out=tile[:, 0 : words.shape[1]], in_=words.rearrange("p c d -> p (c d)").bitcast(I32))
+            nc.sync.dma_start(out=tile[:], in_=words.rearrange("p c d -> p (c d)").bitcast(I32))
 
-        def load_pair(tile, words, a):
+        def load_pair(tiles, words, a):
             nc.sync.dma_start(
-                out=tile[:], in_=words[2 * a : 2 * a + 2, 0].rearrange("e p c d -> p e (c d)").bitcast(I32)
+                out=tiles[a][:], in_=words[2 * a : 2 * a + 2, 0].rearrange("e p c d -> p e (c d)").bitcast(I32)
             )
 
-        def load_wz(e, s):
-            rows = wz[e, s * P * PACK : (s + 1) * P * PACK, :]
-            nc.sync.dma_start(out=raw[e][s][:], in_=rows.rearrange("(p j) c -> p j c", j=PACK))
+        def load_wz(k, h=0):
+            e, s = divmod(k, Z_PASSES)
+            width = raw[k, h].shape[2]
+            rows = wz[e, s * P * PACK : (s + 1) * P * PACK, h * width : (h + 1) * width]
+            nc.sync.dma_start(out=raw[k, h][:], in_=rows.rearrange("(p j) c -> p j c", j=PACK))
+
+        def load_gate1(a):
+            nc.sync.dma_start(out=g1[a][:], in_=gate1[:, 2 * a * C : 2 * (a + 1) * C])
 
         make_identity(nc, ident[:])
-        load_words(xw, x_words[0])
         nc.sync.dma_start(offs_t[:], offs)
-        load_scales(nc.sync, xs, x_scales)
-        load_pair(w1w[0], w1_words, 0)
-        load_words(zw[0], z_words[0])
-        load_scales(nc.sync, w1s, w1_scales[:, 0])
+        load_words(xw, x_words[0])
+        load_scales(xs, x_scales)
         nc.sync.dma_start(offs2_t[:], offs2)
+        load_words(zw[0], z_words[0])
+        load_pair(w1w, w1_words, 0)
+        load_scales(w1s, w1_scales[:, 0])
+        load_wz(0, 0)
         load_words(zw[1], z_words[1])
-        load_pair(w2w[0], w2_words, 0)
-        nc.sync.dma_start(out=g1[:], in_=gate1)
-        load_scales(nc.sync, w2s, w2_scales[:, 0])
-        load_pair(w1w[1], w1_words, 1)
-        load_pair(w2w[1], w2_words, 1)
-        for e in range(2):
-            for s in range(Z_PASSES):
-                load_wz(e, s)
-        load_scales(nc.sync, zs, z_scales)
-        load_wz(2, 0)
+        load_gate1(0)
+        load_scales(w2s, w2_scales[:, 0])
+        load_wz(0, 1)
+        load_pair(w2w, w2_words, 0)
+        load_scales(zs, z_scales)
+        load_wz(1, 0)
+        load_pair(w1w, w1_words, 1)
+        load_wz(1, 1)
+        load_pair(w2w, w2_words, 1)
+        load_wz(2)
+        load_gate1(1)
+        load_wz(3)
         nc.sync.dma_start(out=g2[:], in_=gate2)
-        load_wz(2, 1)
-        load_wz(3, 0)
-        load_wz(3, 1)
+        load_wz(4)
+        load_wz(5)
+        load_wz(6)
+        load_wz(7)
 
-        xg = held([P, E * C], U32, "xg")
-        xgs = held([P, E * C], U8, "xgs")
+        xg = [held([P, 2 * C], U32, "xg%d" % a) for a in range(2)]
+        xgs = [held([P, 2 * C], U8, "xgs%d" % a) for a in range(2)]
         zg = [held([P, E * C], U32, "zg%d" % s) for s in range(Z_PASSES)]
         zgs = held([P, E * C], U8, "zgs")
 
-        def gather_text():
-            nc.vector.tensor_copy(xg[:], xw[:].bitcast(U32).indirect(offs_t[:]))
-            nc.vector.tensor_copy(xgs[:], xs[:].indirect(offs_t[:]))
+        for a in range(2):
+            offsets = offs_t[:, 2 * a * COLS : 2 * (a + 1) * COLS]
+            nc.vector.tensor_copy(xg[a][:], xw[:].bitcast(U32).indirect(offsets))
+            nc.vector.tensor_copy(xgs[a][:], xs[:].indirect(offsets))
+        for s in range(Z_PASSES):
+            nc.vector.tensor_copy(zg[s][:], zw[s][:].bitcast(U32).indirect(offs2_t[:]))
+        nc.vector.tensor_copy(zgs[:], zs[:].indirect(offs2_t[:]))
 
-        def gather_patches():
-            for s in range(Z_PASSES):
-                nc.vector.tensor_copy(zg[s][:], zw[s][:].bitcast(U32).indirect(offs2_t[:]))
-            nc.vector.tensor_copy(zgs[:], zs[:].indirect(offs2_t[:]))
+        def text_rows(a):
+            turn = turned.tile([P, 2, 2, C], F32, name="turn")
+            for i in range(2):
+                e = 2 * a + i
+                slots = slice(i * C, (i + 1) * C)
+                acc = first.tile([P, H], F32, name="acc1")
+                nc.tensor.matmul_mx(
+                    out=acc[:], lhsT=xg[a][:, slots].bitcast(FP8X4), lhsT_scale=xgs[a][:, slots],
+                    rhs=w1w[a][:, i, :].bitcast(FP8X4), rhs_scale=w1s[4 * e :, :], start=True, stop=True,
+                )
+                rows = held([P, H], BF16, "rows%d" % e)
+                nc.scalar.activation(rows[:], acc[:], RELU)
+                pairs = rows[:].bitcast(F32)
+                for u in range(2):
+                    nc.tensor.transpose(turn[:, i, u, :], pairs[:, u : H // 2 : 2], ident[:])
+            return turn
 
-        def text_hidden(e, hidden):
-            slots = slice(e * C, (e + 1) * C)
-            acc = first.tile([P, H], F32, name="acc1")
-            nc.tensor.matmul_mx(
-                out=acc[:], lhsT=xg[:, slots].bitcast(FP8X4), lhsT_scale=xgs[:, slots],
-                rhs=w1w[e // 2][:, e % 2, :].bitcast(FP8X4), rhs_scale=w1s[4 * e :, :], start=True, stop=True,
-            )
-            rows = place([P, H], BF16, "rows%d" % e, rows_at + 1024 if e == E - 1 else None)
-            nc.scalar.activation(rows[:], acc[:], RELU)
-            pairs = rows[:].bitcast(F32)
-            turn = turned.tile([P, 2, C], F32, name="turn")
-            for u in range(2):
-                nc.tensor.transpose(turn[:, u, :], pairs[:, u : H // 2 : 2], ident[:])
-            nc.scalar.copy(
-                hidden.rearrange("p c t -> p (c t)").bitcast(F32).rearrange("p (c u) -> p c u", u=2),
-                turn[:].rearrange("p u c -> p c u"),
-            )
-
-        def patch_hidden(e, quantised, hidden):
-            slots = slice(e * C, (e + 1) * C)
-            acc = first.tile([P, H], F32, name="acc1")
-            for t in range(PACK):
-                cols = slice(t * P, (t + 1) * P)
-                for s, (w, ws) in enumerate(quantised):
-                    nc.tensor.matmul_mx(
-                        out=acc[:, cols], lhsT=w[:, cols].bitcast(FP8X4), lhsT_scale=ws[:, cols],
-                        rhs=zg[s][:, slots].bitcast(FP8X4), rhs_scale=zgs[4 * s :, slots],
-                        start=(s == 0), stop=(s == Z_PASSES - 1),
-                    )
-            nc.scalar.activation(hidden, acc[:].rearrange("p (t c) -> p c t", t=PACK), RELU)
-
-        def second_product(hidden, e0, count, name):
+        def second_product(hidden, e0, count, name, codes_offset=None):
             width = count * C
-            codes = place([P, width], U32, "hcodes" + name, hcodes_at if name == "p3" else None)
+            codes = place([P, width], U32, "hcodes" + name, codes_offset)
             scales = held([P, width], U8, "hscales" + name)
             nc.vector.quantize_mx(
                 out=codes[:].bitcast(FP8X4), scales=scales[:], in_=hidden[:].rearrange("p c t -> p (c t)")
             )
             per_bank = N_TILES // count
-            halves = []
+            banks = []
             for bank in range(count):
                 acc = second.tile([P, per_bank, width], F32, name="acc2")
                 for i in range(count):
@@ -191,79 +188,95 @@ def tile_moe_mmo_relu_kernel(
                             lhsT_scale=w2s[4 * e :, cols], rhs=codes[:, slots].bitcast(FP8X4),
                             rhs_scale=scales[:, slots], start=True, stop=True,
                         )
-                halves += [acc[:, b : b + 2, :] for b in range(0, per_bank, 2)]
-            return halves
+                banks.append(acc)
+            return banks
 
-        def put_back(halves, gate, windows, offsets, e0, half, name, offset):
-            width = halves[half].shape[2]
-            res = place([P, 2, width], F32, "res%s%d" % (name, half), offset)
-            nc.scalar.copy(res[:], halves[half])
-            for b in range(2):
-                nc.vector.tensor_tensor(
-                    windows[2 * half + b][:].indirect(offsets[:, e0 * COLS : e0 * COLS + width // 16]),
-                    res[:, b, :], gate[:, e0 * C : e0 * C + width], MULT,
-                )
-
-        def quantise_wz(e, s, offset=None):
-            shared_cast = offset is not None
-            grouped = place([P, PACK, P, PACK], BF16, "grouped%d%d" % (e, s), offset)
-            dst = grouped[:].rearrange("p t m j -> p m j t")
-            src = raw[e][s][:].rearrange("p j (m t) -> p m j t", t=PACK)
-            last = (e, s) == (E - 1, Z_PASSES - 1)
-            if shared_cast:
-                nc.scalar.copy(dst[:, : P // 2], src[:, : P // 2])
-                nc.vector.tensor_copy(dst[:, P // 2 :], src[:, P // 2 :])
-            else:
-                nc.scalar.copy(dst, src)
-            codes = place([P, H], U32, "wcodes%d%d" % (e, s), codes_at if last else None)
-            scales = held([P, H], U8, "wscales%d%d" % (e, s))
-            nc.vector.quantize_mx(
-                out=codes[:].bitcast(FP8X4), scales=scales[:], in_=grouped[:].rearrange("p t m j -> p (t m j)")
+        def text_sums(a, turn, offset):
+            hidden = place([P, 2 * C, PACK], BF16, "hidden_t%d" % a, offset)
+            nc.scalar.copy(
+                hidden[:].rearrange("p c t -> p (c t)").bitcast(F32).rearrange("p (i c u) -> p i c u", i=2, u=2),
+                turn[:].rearrange("p i u c -> p i c u"),
             )
-            return codes, scales
+            return second_product(hidden, 2 * a, 2, "t%d" % a)
 
-        def text_sums(e0):
-            hidden = held([P, 2 * C, PACK], BF16, "hidden_t%d" % e0)
-            for i in range(2):
-                text_hidden(e0 + i, hidden[:, i * C : (i + 1) * C, :])
-            return second_product(hidden, e0, 2, "t%d" % e0)
+        def patch_sums(e, offset, codes_offset=None):
+            slots = slice(e * C, (e + 1) * C)
+            acc = first.tile([P, H], F32, name="acc1")
+            for t in range(PACK):
+                cols = slice(t * P, (t + 1) * P)
+                for s in range(Z_PASSES):
+                    w, ws = quantised[Z_PASSES * e + s]
+                    nc.tensor.matmul_mx(
+                        out=acc[:, cols], lhsT=w[:, cols].bitcast(FP8X4), lhsT_scale=ws[:, cols],
+                        rhs=zg[s][:, slots].bitcast(FP8X4), rhs_scale=zgs[4 * s :, slots],
+                        start=(s == 0), stop=(s == Z_PASSES - 1),
+                    )
+            hidden = place([P, C, PACK], BF16, "hidden_p%d" % e, offset)
+            nc.scalar.activation(hidden[:], acc[:].rearrange("p (t c) -> p c t", t=PACK), RELU)
+            return second_product(hidden, e, 1, "p%d" % e, codes_offset)
 
-        def patch_sums(e0, quantised, offset):
-            hidden = place([P, len(quantised) * C, PACK], BF16, "hidden_p%d" % e0, offset)
-            for i, passes in enumerate(quantised):
-                patch_hidden(e0 + i, passes, hidden[:, i * C : (i + 1) * C, :])
-            return second_product(hidden, e0, len(quantised), "p%d" % e0)
+        def leave_bank(banks, b0, b1, name, offset):
+            per_bank, width = banks[0].shape[1], banks[0].shape[2]
+            res = place([P, b1 - b0, width], F32, "res%s%d" % (name, b0), offset)
+            nc.scalar.copy(res[:], banks[b0 // per_bank][:, b0 % per_bank : (b1 - 1) % per_bank + 1, :])
+            return {b: res[:, b - b0, :] for b in range(b0, b1)}
 
-        def put_text(halves, e0, half, offset):
-            put_back(halves, g1, text_out, offs_t, e0, half, "t%d" % e0, offset)
+        def scatter(window, offsets, values, gate):
+            nc.vector.tensor_tensor(window[:].indirect(offsets), values, gate, MULT)
 
-        def put_patches(halves, e0, half, offset):
-            put_back(halves, g2, patch_out, offs2_t, e0, half, "p%d" % e0, offset)
+        def put_text(a, sums, blocks=None):
+            for b in blocks or sums:
+                scatter(text_out[b], offs_t[:, 2 * a * COLS : 2 * (a + 1) * COLS], sums[b], g1[a][:])
 
-        gather_text()
-        gather_patches()
-        t01 = text_sums(0)
-        put_text(t01, 0, 0, None)
-        t23 = text_sums(2)
-        put_text(t01, 0, 1, rows_at + 1024)
-        q0 = [quantise_wz(0, 0)]
-        put_text(t23, 2, 0, raw_at(0, 0))
-        q0.append(quantise_wz(0, 1))
-        q1 = [quantise_wz(1, 0), quantise_wz(1, 1)]
-        put_text(t23, 2, 1, raw_at(1, 1))
-        q2 = [quantise_wz(2, 0)]
-        p01 = patch_sums(0, [q0, q1], raw_at(2, 0))
-        q2.append(quantise_wz(2, 1, raw_at(2, 0, 2)))
-        q3 = [quantise_wz(3, 0, raw_at(2, 1))]
-        put_patches(p01, 0, 0, raw_at(3, 0))
-        q3.append(quantise_wz(3, 1))
-        p2 = patch_sums(2, [q2], raw_at(3, 1, 0))
-        put_patches(p01, 0, 1, raw_at(3, 1, 1))
-        p3 = patch_sums(3, [q3], None)
-        put_patches(p2, 2, 0, codes_at)
-        put_patches(p3, 3, 0, None)
-        put_patches(p2, 2, 1, hcodes_at)
-        put_patches(p3, 3, 1, None)
+        def put_patches(e, sums, blocks=None):
+            for b in blocks or sums:
+                scatter(patch_out[b], offs2_t[:, e * COLS : (e + 1) * COLS], sums[b], g2[:, e * C : (e + 1) * C])
+
+        grouped, quantised = {}, {}
+
+        def cast_wz(k, h=0, copy=nc.scalar.copy):
+            if k not in grouped:
+                grouped[k] = held([P, PACK, P, PACK], BF16, "grouped%d" % k)
+            src = raw[k, h][:].rearrange("p j (m t) -> p m j t", t=PACK)
+            count = src.shape[1]
+            copy(grouped[k][:].rearrange("p t m j -> p m j t")[:, h * count : (h + 1) * count], src)
+
+        def quantise_wz(k, codes_offset=None):
+            codes = place([P, H], U32, "wcodes%d" % k, codes_offset)
+            scales = held([P, H], U8, "wscales%d" % k)
+            nc.vector.quantize_mx(
+                out=codes[:].bitcast(FP8X4), scales=scales[:], in_=grouped[k][:].rearrange("p t m j -> p (t m j)")
+            )
+            quantised[k] = codes, scales
+
+        turn = text_rows(0)
+        cast_wz(0, 0)
+        t01 = text_sums(0, turn, None)
+        cast_wz(0, 1)
+        quantise_wz(0)
+        put_text(0, leave_bank(t01, 0, 2, "t0", raw_at(0, 2)))
+        cast_wz(1, 0)
+        turn = text_rows(1)
+        cast_wz(1, 1)
+        quantise_wz(1)
+        t23 = text_sums(1, turn, raw_at(1, 2))
+        put_text(0, leave_bank(t01, 2, 4, "t0", raw_at(1, 3)))
+        for e in range(E - 1):
+            k = Z_PASSES * (e + 1)
+            cast_wz(k)
+            quantise_wz(k)
+            sums = patch_sums(e, raw_at(k, 0))
+            put_text(1, leave_bank(t23, e, e + 1, "t1", raw_at(k, 1)))
+            cast_wz(k + 1)
+            quantise_wz(k + 1, codes_at if e == E - 2 else None)
+            put_patches(e, leave_bank(sums, 0, N_TILES - 1 if e == E - 2 else N_TILES, "p%d" % e, raw_at(k + 1)))
+        last = patch_sums(E - 1, None, hcodes_at)
+        put_text(1, leave_bank(t23, 3, 4, "t1", codes_at))
+        put_patches(3, leave_bank(last, 0, 1, "p3", None))
+        rest = leave_bank(last, 1, 4, "p3", None)
+        put_patches(3, rest, (1,))
+        put_patches(2, leave_bank(sums, 3, 4, "p2", hcodes_at))
+        put_patches(3, rest, (2, 3))
         for b in range(N_TILES):
             nc.sync.dma_start(out=out[b * P : (b + 1) * P, 0:T], in_=text_out[b][:])
         for b in range(N_TILES):

@@ -24,7 +24,7 @@ Z_PASSES = L // (P * PACK)
 N_TILES = N // P
 COLS = C // 16
 PASSES = E * Z_PASSES
-HALVED = (0, 1)
+HALVED = ()
 RAW_BYTES = PACK * H * 4
 PART_BYTES = 2048
 
@@ -110,29 +110,27 @@ def tile_moe_mmo_relu_kernel(
             nc.sync.dma_start(out=g1[a][:], in_=gate1[:, 2 * a * C : 2 * (a + 1) * C])
 
         make_identity(nc, ident[:])
-        nc.sync.dma_start(offs_t[:], offs)
         load_words(xw, x_words[0])
-        load_scales(xs, x_scales)
+        nc.sync.dma_start(offs_t[:], offs)
         nc.sync.dma_start(offs2_t[:], offs2)
-        load_words(zw[0], z_words[0])
+        load_scales(xs, x_scales)
         load_pair(w1w, w1_words, 0)
         load_scales(w1s, w1_scales[:, 0])
-        load_wz(0, 0)
+        load_words(zw[0], z_words[0])
         load_words(zw[1], z_words[1])
-        load_gate1(0)
         load_scales(w2s, w2_scales[:, 0])
-        load_wz(0, 1)
         load_pair(w2w, w2_words, 0)
-        load_scales(zs, z_scales)
-        load_wz(1, 0)
+        load_gate1(0)
+        load_wz(0)
         load_pair(w1w, w1_words, 1)
-        load_wz(1, 1)
-        load_pair(w2w, w2_words, 1)
+        load_wz(1)
+        load_scales(zs, z_scales)
         load_wz(2)
-        load_gate1(1)
+        load_pair(w2w, w2_words, 1)
         load_wz(3)
-        nc.sync.dma_start(out=g2[:], in_=gate2)
+        load_gate1(1)
         load_wz(4)
+        nc.sync.dma_start(out=g2[:], in_=gate2)
         load_wz(5)
         load_wz(6)
         load_wz(7)
@@ -234,12 +232,15 @@ def tile_moe_mmo_relu_kernel(
 
         grouped, quantised = {}, {}
 
-        def cast_wz(k, h=0, copy=nc.scalar.copy):
-            if k not in grouped:
-                grouped[k] = held([P, PACK, P, PACK], BF16, "grouped%d" % k)
-            src = raw[k, h][:].rearrange("p j (m t) -> p m j t", t=PACK)
-            count = src.shape[1]
-            copy(grouped[k][:].rearrange("p t m j -> p m j t")[:, h * count : (h + 1) * count], src)
+        def cast_wz(k, shared_with_vector=False):
+            grouped[k] = held([P, PACK, P, PACK], BF16, "grouped%d" % k)
+            dst = grouped[k][:].rearrange("p t m j -> p m j t")
+            src = raw[k, 0][:].rearrange("p j (m t) -> p m j t", t=PACK)
+            if shared_with_vector:
+                nc.scalar.copy(dst[:, : P // 2], src[:, : P // 2])
+                nc.vector.tensor_copy(dst[:, P // 2 :], src[:, P // 2 :])
+            else:
+                nc.scalar.copy(dst, src)
 
         def quantise_wz(k, codes_offset=None):
             codes = place([P, H], U32, "wcodes%d" % k, codes_offset)
@@ -249,18 +250,15 @@ def tile_moe_mmo_relu_kernel(
             )
             quantised[k] = codes, scales
 
-        turn = text_rows(0)
-        cast_wz(0, 0)
-        t01 = text_sums(0, turn, None)
-        cast_wz(0, 1)
+        t01 = text_sums(0, text_rows(0), None)
+        put_text(0, leave_bank(t01, 0, 2, "t0", None))
+        cast_wz(0)
         quantise_wz(0)
-        put_text(0, leave_bank(t01, 0, 2, "t0", raw_at(0, 2)))
-        cast_wz(1, 0)
         turn = text_rows(1)
-        cast_wz(1, 1)
+        cast_wz(1, shared_with_vector=True)
         quantise_wz(1)
-        t23 = text_sums(1, turn, raw_at(1, 2))
-        put_text(0, leave_bank(t01, 2, 4, "t0", raw_at(1, 3)))
+        t23 = text_sums(1, turn, raw_at(1, 0))
+        put_text(0, leave_bank(t01, 2, 4, "t0", raw_at(1, 1)))
         for e in range(E - 1):
             k = Z_PASSES * (e + 1)
             cast_wz(k)

@@ -259,23 +259,25 @@ def tile_moe_mmo_relu_kernel(
         quantise_wz(1)
         t23 = text_sums(1, turn, raw_at(1, 0))
         put_text(0, leave_bank(t01, 2, 4, "t0", raw_at(1, 1)))
+        sums = {}
         for e in range(E - 1):
             k = Z_PASSES * (e + 1)
             cast_wz(k)
             quantise_wz(k)
-            sums = patch_sums(e, raw_at(k, 0))
+            sums[e] = patch_sums(e, raw_at(k, 0))
             put_text(1, leave_bank(t23, e, e + 1, "t1", raw_at(k, 1)))
             cast_wz(k + 1)
             quantise_wz(k + 1, codes_at if e == E - 2 else None)
-            put_patches(e, leave_bank(sums, 0, N_TILES - 1 if e == E - 2 else N_TILES, "p%d" % e, raw_at(k + 1)))
+            if e == E - 2:
+                put_patches(e - 1, leave_bank(sums[e - 1], 3, 4, "p%d" % (e - 1), raw_at(k + 1, 1)))
+            put_patches(e, leave_bank(sums[e], 0, N_TILES - e, "p%d" % e, raw_at(k + 1)))
         last = patch_sums(E - 1, None, hcodes_at)
-        put_text(1, leave_bank(t23, 3, 4, "t1", codes_at))
+        put_patches(2, leave_bank(sums[2], 2, 4, "p2", codes_at))
         put_patches(3, leave_bank(last, 0, 1, "p3", None))
-        rest = leave_bank(last, 1, 4, "p3", None)
-        put_patches(3, rest, (1,))
-        put_patches(2, leave_bank(sums, 3, 4, "p2", hcodes_at))
-        put_patches(3, rest, (2, 3))
-        for b in range(N_TILES):
+        put_patches(3, leave_bank(last, 1, 4, "p3", None))
+        put_text(1, leave_bank(t23, 3, 4, "t1", hcodes_at))
+        for b in range(N_TILES - 1):
             nc.sync.dma_start(out=out[b * P : (b + 1) * P, 0:T], in_=text_out[b][:])
         for b in range(N_TILES):
             nc.sync.dma_start(out=out[b * P : (b + 1) * P, T : T + Q], in_=patch_out[b][:])
+        nc.sync.dma_start(out=out[(N_TILES - 1) * P :, 0:T], in_=text_out[N_TILES - 1][:])

@@ -54,7 +54,7 @@ def tile_moe_mmo_relu_kernel(
             return k * RAW_BYTES + part * PART_BYTES
 
         codes_at = PASSES * RAW_BYTES
-        hcodes_at = codes_at + PART_BYTES
+        hcodes_at = codes_at + 2 * PART_BYTES
 
         offs_t = held([P, E * COLS], U16, "offs_t")
         offs2_t = held([P, E * COLS], U16, "offs2_t")
@@ -260,22 +260,29 @@ def tile_moe_mmo_relu_kernel(
         t23 = text_sums(1, turn, raw_at(1, 0))
         put_text(0, leave_bank(t01, 2, 4, "t0", raw_at(1, 1)))
         sums = {}
-        for e in range(E - 1):
+        for e in range(E - 2):
             k = Z_PASSES * (e + 1)
             cast_wz(k)
             quantise_wz(k)
             sums[e] = patch_sums(e, raw_at(k, 0))
             put_text(1, leave_bank(t23, e, e + 1, "t1", raw_at(k, 1)))
             cast_wz(k + 1)
-            quantise_wz(k + 1, codes_at if e == E - 2 else None)
-            if e == E - 2:
-                put_patches(e - 1, leave_bank(sums[e - 1], 3, 4, "p%d" % (e - 1), raw_at(k + 1, 1)))
+            quantise_wz(k + 1)
             put_patches(e, leave_bank(sums[e], 0, N_TILES - e, "p%d" % e, raw_at(k + 1)))
+        cast_wz(6)
+        quantise_wz(6)
+        sums[2] = patch_sums(2, raw_at(6, 0))
+        put_patches(1, leave_bank(sums[1], 3, 4, "p1", raw_at(6, 1)))
+        cast_wz(7, shared_with_vector=True)
+        quantise_wz(7, codes_at)
+        put_text(1, leave_bank(t23, 2, 3, "t1", raw_at(7, 0)))
+        put_patches(2, leave_bank(sums[2], 0, 1, "p2", raw_at(7, 1)))
         last = patch_sums(E - 1, None, hcodes_at)
-        put_patches(2, leave_bank(sums[2], 2, 4, "p2", codes_at))
+        put_patches(2, leave_bank(sums[2], 1, 3, "p2", codes_at))
         put_patches(3, leave_bank(last, 0, 1, "p3", None))
+        put_patches(2, leave_bank(sums[2], 3, 4, "p2", hcodes_at + 256))
         put_patches(3, leave_bank(last, 1, 4, "p3", None))
-        put_text(1, leave_bank(t23, 3, 4, "t1", hcodes_at))
+        put_text(1, leave_bank(t23, 3, 4, "t1", hcodes_at + 256 - 2 * C * 4))
         for b in range(N_TILES - 1):
             nc.sync.dma_start(out=out[b * P : (b + 1) * P, 0:T], in_=text_out[b][:])
         for b in range(N_TILES):

@@ -135,18 +135,41 @@ def tile_moe_mmo_relu_kernel(
         load_wz(6)
         load_wz(7)
 
-        xg = [held([P, 2 * C], U32, "xg%d" % a) for a in range(2)]
-        xgs = [held([P, 2 * C], U8, "xgs%d" % a) for a in range(2)]
+        first_hidden_at = hcodes_at + PART_BYTES
+        xg = [held([P, 2 * C], U32, "xg0"), placed([P, 2 * C], U32, "xg1", first_hidden_at)]
+        xgs = [held([P, 2 * C], U8, "xgs0"), placed([P, 2 * C], U8, "xgs1", first_hidden_at + 2 * C * 4)]
         zg = [held([P, E * C], U32, "zg%d" % s) for s in range(Z_PASSES)]
         zgs = held([P, E * C], U8, "zgs")
 
-        for a in range(2):
+        def gather_text(a):
             offsets = offs_t[:, 2 * a * COLS : 2 * (a + 1) * COLS]
             nc.vector.tensor_copy(xg[a][:], xw[:].bitcast(U32).indirect(offsets))
             nc.vector.tensor_copy(xgs[a][:], xs[:].indirect(offsets))
+
+        gather_text(0)
+        w1g = held([P, 2, PACK, P], I32, "w1g")
+        w1gs = held([P, PACK, P], U8, "w1gs")
+        nc.vector.tensor_copy(
+            w1g[:].rearrange("p e t m -> p e m t"), w1w[0][:].rearrange("p e (m t) -> p e m t", t=PACK)
+        )
+        nc.vector.tensor_copy(w1gs[:].rearrange("p t m -> p m t"), w1s[:].rearrange("p (m t) -> p m t", t=PACK))
         for s in range(Z_PASSES):
             nc.vector.tensor_copy(zg[s][:], zw[s][:].bitcast(U32).indirect(offs2_t[:]))
         nc.vector.tensor_copy(zgs[:], zs[:].indirect(offs2_t[:]))
+
+        def first_text_sums():
+            hidden = placed([P, 2 * C, PACK], BF16, "hidden_t0", first_hidden_at)
+            for e in range(2):
+                slots = slice(e * C, (e + 1) * C)
+                acc = first.tile([P, H], F32, name="acc1")
+                for t in range(PACK):
+                    nc.tensor.matmul_mx(
+                        out=acc[:, t * P : (t + 1) * P], lhsT=w1g[:, e, t, :].bitcast(FP8X4),
+                        lhsT_scale=w1gs[4 * e :, t, :], rhs=xg[0][:, slots].bitcast(FP8X4),
+                        rhs_scale=xgs[0][:, slots], start=True, stop=True,
+                    )
+                nc.scalar.activation(hidden[:, slots, :], acc[:].rearrange("p (t c) -> p c t", t=PACK), RELU)
+            return second_product(hidden, 0, 2, "t0")
 
         def text_rows(a):
             turn = turned.tile([P, 2, 2, C], F32, name="turn")
@@ -250,7 +273,8 @@ def tile_moe_mmo_relu_kernel(
             )
             quantised[k] = codes, scales
 
-        t01 = text_sums(0, text_rows(0), None)
+        t01 = first_text_sums()
+        gather_text(1)
         put_text(0, leave_bank(t01, 0, 2, "t0", None))
         cast_wz(0)
         quantise_wz(0)
@@ -279,9 +303,9 @@ def tile_moe_mmo_relu_kernel(
         put_patches(2, leave_bank(sums[2], 0, 1, "p2", raw_at(7, 1)))
         last = patch_sums(E - 1, None, hcodes_at)
         put_patches(2, leave_bank(sums[2], 1, 3, "p2", codes_at))
-        put_patches(3, leave_bank(last, 0, 1, "p3", None))
+        put_patches(3, leave_bank(last, 0, 2, "p3", None))
         put_patches(2, leave_bank(sums[2], 3, 4, "p2", hcodes_at + 256))
-        put_patches(3, leave_bank(last, 1, 4, "p3", None))
+        put_patches(3, leave_bank(last, 2, 4, "p3", None))
         put_text(1, leave_bank(t23, 3, 4, "t1", hcodes_at + 256 - 2 * C * 4))
         for b in range(N_TILES - 1):
             nc.sync.dma_start(out=out[b * P : (b + 1) * P, 0:T], in_=text_out[b][:])

@@ -77,7 +77,9 @@ def tile_moe_mmo_relu_kernel(
         patch_out = [held([P, Q], F32, "patch_out%d" % b) for b in range(N_TILES)]
         ident = held([P, P], F32, "ident")
 
-        for plane in (xs, w1s, w2s, zs):
+        for plane in (xs, w1s):
+            nc.gpsimd.memset(plane[:].bitcast(I32), 0)
+        for plane in (w2s, zs):
             nc.vector.memset(plane[:].bitcast(I32), 0)
         for b in range(2):
             nc.vector.memset(patch_out[b][:], 0.0)
@@ -112,15 +114,15 @@ def tile_moe_mmo_relu_kernel(
         make_identity(nc, ident[:])
         load_words(xw, x_words[0])
         nc.sync.dma_start(offs_t[:], offs)
-        nc.sync.dma_start(offs2_t[:], offs2)
         load_scales(xs, x_scales)
         load_pair(w1w, w1_words, 0)
+        load_gate1(0)
         load_scales(w1s, w1_scales[:, 0])
+        nc.sync.dma_start(offs2_t[:], offs2)
         load_words(zw[0], z_words[0])
         load_words(zw[1], z_words[1])
         load_scales(w2s, w2_scales[:, 0])
         load_pair(w2w, w2_words, 0)
-        load_gate1(0)
         load_wz(0)
         load_pair(w1w, w1_words, 1)
         load_wz(1)
@@ -255,15 +257,13 @@ def tile_moe_mmo_relu_kernel(
 
         grouped, quantised = {}, {}
 
-        def cast_wz(k, shared_with_vector=False):
+        def cast_wz(k, on_scalar=P):
             grouped[k] = held([P, PACK, P, PACK], BF16, "grouped%d" % k)
             dst = grouped[k][:].rearrange("p t m j -> p m j t")
             src = raw[k, 0][:].rearrange("p j (m t) -> p m j t", t=PACK)
-            if shared_with_vector:
-                nc.scalar.copy(dst[:, : P // 2], src[:, : P // 2])
-                nc.vector.tensor_copy(dst[:, P // 2 :], src[:, P // 2 :])
-            else:
-                nc.scalar.copy(dst, src)
+            nc.scalar.copy(dst[:, :on_scalar], src[:, :on_scalar])
+            if on_scalar < P:
+                nc.vector.tensor_copy(dst[:, on_scalar:], src[:, on_scalar:])
 
         def quantise_wz(k, codes_offset=None):
             codes = place([P, H], U32, "wcodes%d" % k, codes_offset)
@@ -279,7 +279,7 @@ def tile_moe_mmo_relu_kernel(
         cast_wz(0)
         quantise_wz(0)
         turn = text_rows(1)
-        cast_wz(1, shared_with_vector=True)
+        cast_wz(1, P // 2)
         quantise_wz(1)
         t23 = text_sums(1, turn, raw_at(1, 0))
         put_text(0, leave_bank(t01, 2, 4, "t0", raw_at(1, 1)))
@@ -297,7 +297,7 @@ def tile_moe_mmo_relu_kernel(
         quantise_wz(6)
         sums[2] = patch_sums(2, raw_at(6, 0))
         put_patches(1, leave_bank(sums[1], 3, 4, "p1", raw_at(6, 1)))
-        cast_wz(7, shared_with_vector=True)
+        cast_wz(7, 5 * P // 8)
         quantise_wz(7, codes_at)
         put_text(1, leave_bank(t23, 2, 3, "t1", raw_at(7, 0)))
         put_patches(2, leave_bank(sums[2], 0, 1, "p2", raw_at(7, 1)))

@@ -1,7 +1,6 @@
 from contextlib import ExitStack
 
 import concourse.mybir as mybir
-from concourse.masks import make_identity
 
 K, L, T, Q, E, C = 512, 1024, 512, 1024, 4, 128
 H, N = 512, 512
@@ -15,6 +14,7 @@ U16 = mybir.dt.uint16
 U8 = mybir.dt.uint8
 FP8X4 = mybir.dt.float8_e4m3fn_x4
 RELU = mybir.ActivationFunctionType.Relu
+COPY = mybir.ActivationFunctionType.Copy
 MULT = mybir.AluOpType.mult
 
 P = 128
@@ -24,9 +24,8 @@ Z_PASSES = L // (P * PACK)
 N_TILES = N // P
 COLS = C // 16
 PASSES = E * Z_PASSES
-HALVED = ()
 RAW_BYTES = PACK * H * 4
-PART_BYTES = 2048
+BANK_BYTES = 2048
 
 
 def tile_moe_mmo_relu_kernel(
@@ -36,25 +35,23 @@ def tile_moe_mmo_relu_kernel(
     nc = tc.nc
     with ExitStack() as ctx:
         keep = ctx.enter_context(tc.tile_pool(name="keep", bufs=1))
-        first = ctx.enter_context(tc.psum_pool(name="first", bufs=2))
-        turned = ctx.enter_context(tc.psum_pool(name="turned", bufs=2))
-        second = ctx.enter_context(tc.psum_pool(name="second", bufs=4))
+        psum = ctx.enter_context(tc.psum_pool(name="psum", bufs=1))
+
         shared = ctx.enter_context(tc.tile_pool(name="shared", bufs=1))
 
-        def held(shape, dtype, name):
-            return keep.tile(shape, dtype, name=name, align_bytes=64)
-
-        def placed(shape, dtype, name, offset):
+        def held(shape, dtype, name, offset=None):
+            if offset is None:
+                return keep.tile(shape, dtype, name=name, align_bytes=64)
             return shared.tile(shape, dtype, name=name, offset=offset, align_bytes=64)
 
-        def place(shape, dtype, name, offset):
-            return held(shape, dtype, name) if offset is None else placed(shape, dtype, name, offset)
+        def bank_tile(shape, name, bank):
+            return psum.tile(shape, F32, name=name, offset=bank * BANK_BYTES)
 
-        def raw_at(k, part=0):
-            return k * RAW_BYTES + part * PART_BYTES
+        def raw_at(k):
+            return k * RAW_BYTES
 
-        codes_at = PASSES * RAW_BYTES
-        hcodes_at = codes_at + 2 * PART_BYTES
+        def grouped_at(k):
+            return PASSES * RAW_BYTES + E * C + k * RAW_BYTES // 2
 
         offs_t = held([P, E * COLS], U16, "offs_t")
         offs2_t = held([P, E * COLS], U16, "offs2_t")
@@ -63,19 +60,14 @@ def tile_moe_mmo_relu_kernel(
         zw = [held([P, Q], I32, "zw%d" % s) for s in range(Z_PASSES)]
         zs = held([P, Q], U8, "zs")
         w1w = [held([P, 2, H], I32, "w1w%d" % a) for a in range(2)]
-        w2w = [held([P, 2, N], I32, "w2w%d" % a) for a in range(2)]
+        w2w = [held([P, 2, N], I32, "w2w0"), held([P, 2, N], I32, "w2w1", grouped_at(PASSES))]
         w1s = held([P, H], U8, "w1s")
         w2s = held([P, N], U8, "w2s")
         g1 = [held([P, 2 * C], F32, "g1%d" % a) for a in range(2)]
         g2 = held([P, E * C], F32, "g2")
-        raw = {}
-        for k in range(PASSES):
-            parts = 2 if k in HALVED else 1
-            for h in range(parts):
-                raw[k, h] = placed([P, PACK, H // parts], F32, "raw%d%d" % (k, h), raw_at(k, 2 * h))
+        raw = [held([P, PACK, H], F32, "raw%d" % k, raw_at(k)) for k in range(PASSES)]
         text_out = [held([P, T], F32, "text_out%d" % b) for b in range(N_TILES)]
         patch_out = [held([P, Q], F32, "patch_out%d" % b) for b in range(N_TILES)]
-        ident = held([P, P], F32, "ident")
 
         for plane in (xs, w1s):
             nc.gpsimd.memset(plane[:].bitcast(I32), 0)
@@ -86,10 +78,10 @@ def tile_moe_mmo_relu_kernel(
         for b in range(2, N_TILES):
             nc.scalar.activation(patch_out[b][:], patch_out[0][:], RELU)
 
-        def load_scales(plane, rows, queue=nc.sync):
+        def load_scales(plane, rows):
             count = rows.shape[0]
             for q in range(QUADS):
-                queue.dma_start(
+                nc.sync.dma_start(
                     out=plane[32 * q : 32 * q + 4 * count, :].bitcast(I32),
                     in_=rows[:, 4 * q : 4 * q + 4, :].bitcast(I32),
                 )
@@ -102,105 +94,111 @@ def tile_moe_mmo_relu_kernel(
                 out=tiles[a][:], in_=words[2 * a : 2 * a + 2, 0].rearrange("e p c d -> p e (c d)").bitcast(I32)
             )
 
-        def load_wz(k, h=0):
+        def load_wz(k):
             e, s = divmod(k, Z_PASSES)
-            width = raw[k, h].shape[2]
-            rows = wz[e, s * P * PACK : (s + 1) * P * PACK, h * width : (h + 1) * width]
-            nc.sync.dma_start(out=raw[k, h][:], in_=rows.rearrange("(p j) c -> p j c", j=PACK))
+            rows = wz[e, s * P * PACK : (s + 1) * P * PACK, :]
+            nc.sync.dma_start(out=raw[k][:], in_=rows.rearrange("(p j) c -> p j c", j=PACK))
 
         def load_gate1(a):
             nc.sync.dma_start(out=g1[a][:], in_=gate1[:, 2 * a * C : 2 * (a + 1) * C])
 
-        make_identity(nc, ident[:])
         load_words(xw, x_words[0])
         nc.sync.dma_start(offs_t[:], offs)
         load_scales(xs, x_scales)
         load_pair(w1w, w1_words, 0)
-        load_gate1(0)
+        load_pair(w1w, w1_words, 1)
         load_scales(w1s, w1_scales[:, 0])
         nc.sync.dma_start(offs2_t[:], offs2)
         load_words(zw[0], z_words[0])
         load_words(zw[1], z_words[1])
-        load_scales(w2s, w2_scales[:, 0])
         load_pair(w2w, w2_words, 0)
+        load_scales(w2s, w2_scales[:, 0])
+        load_gate1(0)
         load_wz(0)
-        load_pair(w1w, w1_words, 1)
-        load_wz(1)
         load_scales(zs, z_scales)
-        load_wz(2)
-        load_pair(w2w, w2_words, 1)
-        load_wz(3)
-        load_gate1(1)
-        load_wz(4)
+        load_wz(1)
         nc.sync.dma_start(out=g2[:], in_=gate2)
+        load_wz(2)
+        load_wz(3)
+        load_wz(4)
+        load_pair(w2w, w2_words, 1)
         load_wz(5)
         load_wz(6)
         load_wz(7)
+        load_gate1(1)
 
-        first_hidden_at = hcodes_at + PART_BYTES
-        xg = [held([P, 2 * C], U32, "xg0"), placed([P, 2 * C], U32, "xg1", first_hidden_at)]
-        xgs = [held([P, 2 * C], U8, "xgs0"), placed([P, 2 * C], U8, "xgs1", first_hidden_at + 2 * C * 4)]
+        xg = [held([P, 2 * C], U32, "xg%d" % a) for a in range(2)]
+        xgs = [held([P, 2 * C], U8, "xgs%d" % a) for a in range(2)]
         zg = [held([P, E * C], U32, "zg%d" % s) for s in range(Z_PASSES)]
         zgs = held([P, E * C], U8, "zgs")
+        w1g = [held([P, 2, PACK, P], U32, "w1g%d" % a) for a in range(2)]
+        w1gs = held([P, PACK, P], U8, "w1gs")
 
         def gather_text(a):
             offsets = offs_t[:, 2 * a * COLS : 2 * (a + 1) * COLS]
             nc.vector.tensor_copy(xg[a][:], xw[:].bitcast(U32).indirect(offsets))
             nc.vector.tensor_copy(xgs[a][:], xs[:].indirect(offsets))
 
-        gather_text(0)
-        w1g = held([P, 2, PACK, P], I32, "w1g")
-        w1gs = held([P, PACK, P], U8, "w1gs")
-        nc.vector.tensor_copy(
-            w1g[:].rearrange("p e t m -> p e m t"), w1w[0][:].rearrange("p e (m t) -> p e m t", t=PACK)
-        )
-        nc.vector.tensor_copy(w1gs[:].rearrange("p t m -> p m t"), w1s[:].rearrange("p (m t) -> p m t", t=PACK))
-        for s in range(Z_PASSES):
-            nc.vector.tensor_copy(zg[s][:], zw[s][:].bitcast(U32).indirect(offs2_t[:]))
-        nc.vector.tensor_copy(zgs[:], zs[:].indirect(offs2_t[:]))
-
-        def first_text_sums():
-            hidden = placed([P, 2 * C, PACK], BF16, "hidden_t0", first_hidden_at)
-            for e in range(2):
-                slots = slice(e * C, (e + 1) * C)
-                acc = first.tile([P, H], F32, name="acc1")
-                for t in range(PACK):
-                    nc.tensor.matmul_mx(
-                        out=acc[:, t * P : (t + 1) * P], lhsT=w1g[:, e, t, :].bitcast(FP8X4),
-                        lhsT_scale=w1gs[4 * e :, t, :], rhs=xg[0][:, slots].bitcast(FP8X4),
-                        rhs_scale=xgs[0][:, slots], start=True, stop=True,
+        def regroup_w1(a, on_scalar):
+            for i in range(2):
+                if on_scalar:
+                    nc.scalar.copy(
+                        w1g[a][:, i].rearrange("p t m -> p m t"),
+                        w1w[a][:, i, :].bitcast(U32).rearrange("p (m t) -> p m t", t=PACK),
                     )
-                nc.scalar.activation(hidden[:, slots, :], acc[:].rearrange("p (t c) -> p c t", t=PACK), RELU)
-            return second_product(hidden, 0, 2, "t0")
+                else:
+                    nc.vector.tensor_copy(
+                        w1g[a][:, i].bitcast(I32).rearrange("p t m -> p m t"),
+                        w1w[a][:, i, :].rearrange("p (m t) -> p m t", t=PACK),
+                    )
 
-        def text_rows(a):
-            turn = turned.tile([P, 2, 2, C], F32, name="turn")
+        def text_hidden(a, offset):
+            hidden = held([P, 2 * C, PACK], BF16, "hidden_t%d" % a, offset)
             for i in range(2):
                 e = 2 * a + i
                 slots = slice(i * C, (i + 1) * C)
-                acc = first.tile([P, H], F32, name="acc1")
-                nc.tensor.matmul_mx(
-                    out=acc[:], lhsT=xg[a][:, slots].bitcast(FP8X4), lhsT_scale=xgs[a][:, slots],
-                    rhs=w1w[a][:, i, :].bitcast(FP8X4), rhs_scale=w1s[4 * e :, :], start=True, stop=True,
-                )
-                rows = held([P, H], BF16, "rows%d" % e)
-                nc.scalar.activation(rows[:], acc[:], RELU)
-                pairs = rows[:].bitcast(F32)
-                for u in range(2):
-                    nc.tensor.transpose(turn[:, i, u, :], pairs[:, u : H // 2 : 2], ident[:])
-            return turn
+                acc = bank_tile([P, H], "acc_t%d" % e, e)
+                for t in range(PACK):
+                    nc.tensor.matmul_mx(
+                        out=acc[:, t * P : (t + 1) * P], lhsT=w1g[a][:, i, t, :].bitcast(FP8X4),
+                        lhsT_scale=w1gs[4 * e :, t, :], rhs=xg[a][:, slots].bitcast(FP8X4),
+                        rhs_scale=xgs[a][:, slots], start=True, stop=True,
+                    )
+                nc.scalar.activation(hidden[:, slots, :], acc[:].rearrange("p (t c) -> p c t", t=PACK), RELU)
+            return hidden
 
-        def second_product(hidden, e0, count, name, codes_offset=None):
-            width = count * C
-            codes = place([P, width], U32, "hcodes" + name, codes_offset)
+        def patch_hidden(e):
+            slots = slice(e * C, (e + 1) * C)
+            acc = bank_tile([P, H], "acc_p%d" % e, e % 2)
+            for s in range(Z_PASSES):
+                w, ws = quantised[Z_PASSES * e + s]
+                for t in range(PACK):
+                    cols = slice(t * P, (t + 1) * P)
+                    nc.tensor.matmul_mx(
+                        out=acc[:, cols], lhsT=w[:, cols].bitcast(FP8X4), lhsT_scale=ws[:, cols],
+                        rhs=zg[s][:, slots].bitcast(FP8X4), rhs_scale=zgs[4 * s :, slots],
+                        start=(s == 0 and t == 0), stop=(s == Z_PASSES - 1 and t == PACK - 1),
+                    )
+            hidden = held([P, C, PACK], BF16, "hidden_p%d" % e)
+            nc.scalar.activation(hidden[:], acc[:].rearrange("p (t c) -> p c t", t=PACK), RELU)
+            return hidden
+
+        def quantise_hidden(hidden, name, offset=None):
+            width = hidden.shape[1]
+            codes = held([P, width], U32, "hcodes" + name, offset)
             scales = held([P, width], U8, "hscales" + name)
             nc.vector.quantize_mx(
                 out=codes[:].bitcast(FP8X4), scales=scales[:], in_=hidden[:].rearrange("p c t -> p (c t)")
             )
+            return codes, scales
+
+        def second_product(operand, e0, count, name, first_bank):
+            codes, scales = operand
+            width = count * C
             per_bank = N_TILES // count
             banks = []
             for bank in range(count):
-                acc = second.tile([P, per_bank, width], F32, name="acc2")
+                acc = bank_tile([P, per_bank, width], "sums%s%d" % (name, bank), first_bank + bank)
                 for i in range(count):
                     e = e0 + i
                     slots = slice(i * C, (i + 1) * C)
@@ -214,101 +212,108 @@ def tile_moe_mmo_relu_kernel(
                 banks.append(acc)
             return banks
 
-        def text_sums(a, turn, offset):
-            hidden = place([P, 2 * C, PACK], BF16, "hidden_t%d" % a, offset)
-            nc.scalar.copy(
-                hidden[:].rearrange("p c t -> p (c t)").bitcast(F32).rearrange("p (i c u) -> p i c u", i=2, u=2),
-                turn[:].rearrange("p i u c -> p i c u"),
-            )
-            return second_product(hidden, 2 * a, 2, "t%d" % a)
-
-        def patch_sums(e, offset, codes_offset=None):
-            slots = slice(e * C, (e + 1) * C)
-            acc = first.tile([P, H], F32, name="acc1")
-            for t in range(PACK):
-                cols = slice(t * P, (t + 1) * P)
-                for s in range(Z_PASSES):
-                    w, ws = quantised[Z_PASSES * e + s]
-                    nc.tensor.matmul_mx(
-                        out=acc[:, cols], lhsT=w[:, cols].bitcast(FP8X4), lhsT_scale=ws[:, cols],
-                        rhs=zg[s][:, slots].bitcast(FP8X4), rhs_scale=zgs[4 * s :, slots],
-                        start=(s == 0), stop=(s == Z_PASSES - 1),
-                    )
-            hidden = place([P, C, PACK], BF16, "hidden_p%d" % e, offset)
-            nc.scalar.activation(hidden[:], acc[:].rearrange("p (t c) -> p c t", t=PACK), RELU)
-            return second_product(hidden, e, 1, "p%d" % e, codes_offset)
-
-        def leave_bank(banks, b0, b1, name, offset):
-            per_bank, width = banks[0].shape[1], banks[0].shape[2]
-            res = place([P, b1 - b0, width], F32, "res%s%d" % (name, b0), offset)
-            nc.scalar.copy(res[:], banks[b0 // per_bank][:, b0 % per_bank : (b1 - 1) % per_bank + 1, :])
+        def gated(bank, b0, b1, gate, name, offset=None, res=None):
+            shape = [P, b1 - b0, bank.shape[2]]
+            if res is None:
+                tile = held(shape, F32, "res%s%d" % (name, b0), offset)
+                res = tile[:]
+            nc.vector.tensor_tensor(res, bank[:, b0:b1, :], gate.unsqueeze(1).to_broadcast(shape), MULT)
             return {b: res[:, b - b0, :] for b in range(b0, b1)}
 
-        def scatter(window, offsets, values, gate):
-            nc.vector.tensor_tensor(window[:].indirect(offsets), values, gate, MULT)
+        def gated_text(a, banks, b0, b1, offset=None, res=None):
+            i = b0 // 2
+            res = gated(banks[i], b0 - 2 * i, b1 - 2 * i, g1[a][:], "t%d%d" % (a, i), offset, res)
+            return {2 * i + b: v for b, v in res.items()}
 
-        def put_text(a, sums, blocks=None):
-            for b in blocks or sums:
-                scatter(text_out[b], offs_t[:, 2 * a * COLS : 2 * (a + 1) * COLS], sums[b], g1[a][:])
+        def gated_patches(e, bank, b0, b1, offset=None):
+            return gated(bank, b0, b1, g2[:, e * C : (e + 1) * C], "p%d" % e, offset)
 
-        def put_patches(e, sums, blocks=None):
-            for b in blocks or sums:
-                scatter(patch_out[b], offs2_t[:, e * COLS : (e + 1) * COLS], sums[b], g2[:, e * C : (e + 1) * C])
+        def scatter(window, offsets, values, on_scalar):
+            if on_scalar:
+                nc.scalar.activation(window[:].indirect(offsets), values, COPY)
+            else:
+                nc.vector.tensor_copy(window[:].indirect(offsets), values)
+
+        def put_text(a, res, blocks, on_scalar=True):
+            for b in blocks:
+                scatter(text_out[b], offs_t[:, 2 * a * COLS : 2 * (a + 1) * COLS], res[b], on_scalar)
+
+        def put_patches(e, res, blocks, on_scalar=True):
+            for b in blocks:
+                scatter(patch_out[b], offs2_t[:, e * COLS : (e + 1) * COLS], res[b], on_scalar)
 
         grouped, quantised = {}, {}
 
-        def cast_wz(k, on_scalar=P):
-            grouped[k] = held([P, PACK, P, PACK], BF16, "grouped%d" % k)
+        def cast_wz(k, on_scalar=0):
+            grouped[k] = held([P, PACK, P, PACK], BF16, "grouped%d" % k, grouped_at(k))
             dst = grouped[k][:].rearrange("p t m j -> p m j t")
-            src = raw[k, 0][:].rearrange("p j (m t) -> p m j t", t=PACK)
-            nc.scalar.copy(dst[:, :on_scalar], src[:, :on_scalar])
-            if on_scalar < P:
-                nc.vector.tensor_copy(dst[:, on_scalar:], src[:, on_scalar:])
+            src = raw[k][:].rearrange("p j (m t) -> p m j t", t=PACK)
+            if on_scalar:
+                nc.scalar.copy(dst[:, :on_scalar], src[:, :on_scalar])
+            nc.vector.tensor_copy(dst[:, on_scalar:], src[:, on_scalar:])
 
-        def quantise_wz(k, codes_offset=None):
-            codes = place([P, H], U32, "wcodes%d" % k, codes_offset)
+        def quantise_wz(k):
+            codes = held([P, H], U32, "wcodes%d" % k)
             scales = held([P, H], U8, "wscales%d" % k)
             nc.vector.quantize_mx(
                 out=codes[:].bitcast(FP8X4), scales=scales[:], in_=grouped[k][:].rearrange("p t m j -> p (t m j)")
             )
             quantised[k] = codes, scales
 
-        t01 = first_text_sums()
-        gather_text(1)
-        put_text(0, leave_bank(t01, 0, 2, "t0", None))
-        cast_wz(0)
-        quantise_wz(0)
-        turn = text_rows(1)
-        cast_wz(1, P // 2)
-        quantise_wz(1)
-        t23 = text_sums(1, turn, raw_at(1, 0))
-        put_text(0, leave_bank(t01, 2, 4, "t0", raw_at(1, 1)))
-        sums = {}
-        for e in range(E - 2):
-            k = Z_PASSES * (e + 1)
-            cast_wz(k)
-            quantise_wz(k)
-            sums[e] = patch_sums(e, raw_at(k, 0))
-            put_text(1, leave_bank(t23, e, e + 1, "t1", raw_at(k, 1)))
-            cast_wz(k + 1)
-            quantise_wz(k + 1)
-            put_patches(e, leave_bank(sums[e], 0, N_TILES - e, "p%d" % e, raw_at(k + 1)))
-        cast_wz(6)
-        quantise_wz(6)
-        sums[2] = patch_sums(2, raw_at(6, 0))
-        put_patches(1, leave_bank(sums[1], 3, 4, "p1", raw_at(6, 1)))
-        cast_wz(7, 5 * P // 8)
-        quantise_wz(7, codes_at)
-        put_text(1, leave_bank(t23, 2, 3, "t1", raw_at(7, 0)))
-        put_patches(2, leave_bank(sums[2], 0, 1, "p2", raw_at(7, 1)))
-        last = patch_sums(E - 1, None, hcodes_at)
-        put_patches(2, leave_bank(sums[2], 1, 3, "p2", codes_at))
-        put_patches(3, leave_bank(last, 0, 2, "p3", None))
-        put_patches(2, leave_bank(sums[2], 3, 4, "p2", hcodes_at + 256))
-        put_patches(3, leave_bank(last, 2, 4, "p3", None))
-        put_text(1, leave_bank(t23, 3, 4, "t1", hcodes_at + 256 - 2 * C * 4))
-        for b in range(N_TILES - 1):
+        def store_text(b):
             nc.sync.dma_start(out=out[b * P : (b + 1) * P, 0:T], in_=text_out[b][:])
-        for b in range(N_TILES):
+
+        def store_patches(b):
             nc.sync.dma_start(out=out[b * P : (b + 1) * P, T : T + Q], in_=patch_out[b][:])
-        nc.sync.dma_start(out=out[(N_TILES - 1) * P :, 0:T], in_=text_out[N_TILES - 1][:])
+
+        gather_text(0)
+        regroup_w1(0, True)
+        nc.vector.tensor_copy(w1gs[:].rearrange("p t m -> p m t"), w1s[:].rearrange("p (m t) -> p m t", t=PACK))
+        gather_text(1)
+        regroup_w1(1, True)
+        hidden_text = [text_hidden(a, None) for a in range(2)]
+        for s in range(Z_PASSES):
+            nc.vector.tensor_copy(zg[s][:], zw[s][:].bitcast(U32).indirect(offs2_t[:]))
+        banks = second_product(quantise_hidden(hidden_text[0], "t0"), 0, 2, "t0", 2)
+        late_codes = quantise_hidden(hidden_text[1], "t1")
+        put_text(0, gated_text(0, banks, 0, 1), (0,))
+        cast_wz(0)
+        nc.vector.tensor_copy(zgs[:], zs[:].indirect(offs2_t[:]))
+        quantise_wz(0)
+        cast_wz(1, P // 2)
+        put_text(0, gated_text(0, banks, 1, 2, None, raw[1][:, 0:1, 0 : 2 * C]), (1,))
+        quantise_wz(1)
+        hidden = patch_hidden(0)
+        sums = {}
+        for e in range(1, E):
+            k = Z_PASSES * e
+            cast_wz(k)
+            if e == 1:
+                put_text(0, gated_text(0, banks, 2, 4, raw_at(k)), (2, 3))
+            else:
+                put_patches(e - 2, gated_patches(e - 2, sums[e - 2], 1, 4, raw_at(k)), (1, 2, 3))
+            quantise_wz(k)
+            sums[e - 1] = second_product(quantise_hidden(hidden, "p%d" % (e - 1)), e - 1, 1, "p%d" % (e - 1), 4 + (e - 1) % 2)[0]
+            cast_wz(k + 1)
+            count = 2 if e == E - 1 else 1
+            put_patches(e - 1, gated_patches(e - 1, sums[e - 1], 0, count), range(count))
+            quantise_wz(k + 1)
+            hidden = patch_hidden(e)
+        banks = second_product(late_codes, 2, 2, "t1", 6)
+        rest = gated_patches(2, sums[2], 2, 4, grouped_at(PASSES - 1))
+        put_text(1, gated_text(1, banks, 0, 1, grouped_at(PASSES - 1) + 2 * C * 4), (0,))
+        put_patches(2, rest, (3,), False)
+        last = second_product(quantise_hidden(hidden, "p3"), 3, 1, "p3", 5)[0]
+        put_patches(3, gated_patches(3, last, 0, 2), (0, 1))
+        res = gated_patches(3, last, 2, 4)
+        put_text(1, gated_text(1, banks, 1, 2, grouped_at(PASSES)), (1,))
+        put_patches(3, res, (2, 3), False)
+        late = gated_text(1, banks, 2, 4, grouped_at(PASSES) + 2 * C * 4)
+        put_patches(2, rest, (2,), False)
+        put_text(1, late, (2,))
+        put_text(1, late, (3,), False)
+        store_text(0)
+        for b in (0, 1, 3, 2):
+            store_patches(b)
+        for b in (1, 2, 3):
+            store_text(b)

@@ -26,6 +26,7 @@ COLS = C // 16
 PASSES = E * Z_PASSES
 RAW_BYTES = PACK * H * 4
 BANK_BYTES = 2048
+W2_LOADS = ((0, 2), (2, 1), (3, 1))
 
 
 def tile_moe_mmo_relu_kernel(
@@ -60,7 +61,8 @@ def tile_moe_mmo_relu_kernel(
         zw = [held([P, Q], I32, "zw%d" % s) for s in range(Z_PASSES)]
         zs = held([P, Q], U8, "zs")
         w1w = [held([P, 2, H], I32, "w1w%d" % a) for a in range(2)]
-        w2w = [held([P, 2, N], I32, "w2w0"), held([P, 2, N], I32, "w2w1", grouped_at(PASSES))]
+        w2w = [held([P, count, N], I32, "w2w%d" % e) for e, count in W2_LOADS]
+        w2_of = {e0 + i: w2w[n][:, i, :] for n, (e0, count) in enumerate(W2_LOADS) for i in range(count)}
         w1s = held([P, H], U8, "w1s")
         w2s = held([P, N], U8, "w2s")
         g1 = [held([P, 2 * C], F32, "g1%d" % a) for a in range(2)]
@@ -94,6 +96,12 @@ def tile_moe_mmo_relu_kernel(
                 out=tiles[a][:], in_=words[2 * a : 2 * a + 2, 0].rearrange("e p c d -> p e (c d)").bitcast(I32)
             )
 
+        def load_w2(n):
+            e0, count = W2_LOADS[n]
+            nc.sync.dma_start(
+                out=w2w[n][:], in_=w2_words[e0 : e0 + count, 0].rearrange("e p c d -> p e (c d)").bitcast(I32)
+            )
+
         def load_wz(k):
             e, s = divmod(k, Z_PASSES)
             rows = wz[e, s * P * PACK : (s + 1) * P * PACK, :]
@@ -106,14 +114,13 @@ def tile_moe_mmo_relu_kernel(
         nc.sync.dma_start(offs_t[:], offs)
         load_scales(xs, x_scales)
         load_pair(w1w, w1_words, 0)
-        load_pair(w1w, w1_words, 1)
+        load_gate1(0)
         load_scales(w1s, w1_scales[:, 0])
         nc.sync.dma_start(offs2_t[:], offs2)
         load_words(zw[0], z_words[0])
         load_words(zw[1], z_words[1])
-        load_pair(w2w, w2_words, 0)
+        load_w2(0)
         load_scales(w2s, w2_scales[:, 0])
-        load_gate1(0)
         load_wz(0)
         load_scales(zs, z_scales)
         load_wz(1)
@@ -121,17 +128,19 @@ def tile_moe_mmo_relu_kernel(
         load_wz(2)
         load_wz(3)
         load_wz(4)
-        load_pair(w2w, w2_words, 1)
+        load_w2(1)
         load_wz(5)
         load_wz(6)
         load_wz(7)
+        load_w2(2)
+        load_pair(w1w, w1_words, 1)
         load_gate1(1)
 
         xg = [held([P, 2 * C], U32, "xg%d" % a) for a in range(2)]
         xgs = [held([P, 2 * C], U8, "xgs%d" % a) for a in range(2)]
         zg = [held([P, E * C], U32, "zg%d" % s) for s in range(Z_PASSES)]
         zgs = held([P, E * C], U8, "zgs")
-        w1g = [held([P, 2, PACK, P], U32, "w1g%d" % a) for a in range(2)]
+        w1g = [held([P, 2, PACK, P], U32, "w1g0"), held([P, 2, PACK, P], U32, "w1g1", grouped_at(PASSES - 1))]
         w1gs = held([P, PACK, P], U8, "w1gs")
 
         def gather_text(a):
@@ -157,7 +166,7 @@ def tile_moe_mmo_relu_kernel(
             for i in range(2):
                 e = 2 * a + i
                 slots = slice(i * C, (i + 1) * C)
-                acc = bank_tile([P, H], "acc_t%d" % e, e)
+                acc = bank_tile([P, H], "acc_t%d" % e, 6 * a + i)
                 for t in range(PACK):
                     nc.tensor.matmul_mx(
                         out=acc[:, t * P : (t + 1) * P], lhsT=w1g[a][:, i, t, :].bitcast(FP8X4),
@@ -205,7 +214,7 @@ def tile_moe_mmo_relu_kernel(
                     for b in range(per_bank):
                         cols = slice((bank * per_bank + b) * P, (bank * per_bank + b + 1) * P)
                         nc.tensor.matmul_mx(
-                            out=acc[:, b, slots], lhsT=w2w[e // 2][:, e % 2, cols].bitcast(FP8X4),
+                            out=acc[:, b, slots], lhsT=w2_of[e][:, cols].bitcast(FP8X4),
                             lhsT_scale=w2s[4 * e :, cols], rhs=codes[:, slots].bitcast(FP8X4),
                             rhs_scale=scales[:, slots], start=True, stop=True,
                         )
@@ -270,12 +279,10 @@ def tile_moe_mmo_relu_kernel(
         regroup_w1(0, True)
         nc.vector.tensor_copy(w1gs[:].rearrange("p t m -> p m t"), w1s[:].rearrange("p (m t) -> p m t", t=PACK))
         gather_text(1)
-        regroup_w1(1, True)
-        hidden_text = [text_hidden(a, None) for a in range(2)]
+        hidden = text_hidden(0, None)
         for s in range(Z_PASSES):
             nc.vector.tensor_copy(zg[s][:], zw[s][:].bitcast(U32).indirect(offs2_t[:]))
-        banks = second_product(quantise_hidden(hidden_text[0], "t0"), 0, 2, "t0", 2)
-        late_codes = quantise_hidden(hidden_text[1], "t1")
+        banks = second_product(quantise_hidden(hidden, "t0"), 0, 2, "t0", 2)
         put_text(0, gated_text(0, banks, 0, 1), (0,))
         cast_wz(0)
         nc.vector.tensor_copy(zgs[:], zs[:].indirect(offs2_t[:]))
@@ -299,21 +306,21 @@ def tile_moe_mmo_relu_kernel(
             put_patches(e - 1, gated_patches(e - 1, sums[e - 1], 0, count), range(count))
             quantise_wz(k + 1)
             hidden = patch_hidden(e)
-        banks = second_product(late_codes, 2, 2, "t1", 6)
-        rest = gated_patches(2, sums[2], 2, 4, grouped_at(PASSES - 1))
-        put_text(1, gated_text(1, banks, 0, 1, grouped_at(PASSES - 1) + 2 * C * 4), (0,))
-        put_patches(2, rest, (3,), False)
+        rest = gated_patches(2, sums[2], 2, 4, raw_at(PASSES - 1))
+        regroup_w1(1, False)
         last = second_product(quantise_hidden(hidden, "p3"), 3, 1, "p3", 5)[0]
+        put_patches(2, rest, (3,), False)
+        hidden = text_hidden(1, None)
         put_patches(3, gated_patches(3, last, 0, 2), (0, 1))
+        banks = second_product(quantise_hidden(hidden, "t1"), 2, 2, "t1", 2)
         res = gated_patches(3, last, 2, 4)
-        put_text(1, gated_text(1, banks, 1, 2, grouped_at(PASSES)), (1,))
-        put_patches(3, res, (2, 3), False)
-        late = gated_text(1, banks, 2, 4, grouped_at(PASSES) + 2 * C * 4)
-        put_patches(2, rest, (2,), False)
-        put_text(1, late, (2,))
-        put_text(1, late, (3,), False)
-        store_text(0)
+        put_patches(3, res, (2,), False)
+        put_patches(2, rest, (2,))
+        early = gated_text(1, banks, 0, 2)
+        put_patches(3, res, (3,), False)
+        put_text(1, early, (0, 1))
+        put_text(1, gated_text(1, banks, 2, 4), (3, 2), False)
         for b in (0, 1, 3, 2):
             store_patches(b)
-        for b in (1, 2, 3):
+        for b in (0, 3, 1, 2):
             store_text(b)

@@ -1,6 +1,7 @@
 from contextlib import ExitStack
 
 import concourse.mybir as mybir
+from concourse.masks import make_identity
 
 K, L, T, Q, E, C = 512, 1024, 512, 1024, 4, 128
 H, N = 512, 512
@@ -65,14 +66,20 @@ def tile_moe_mmo_relu_kernel(
         w2_of = {e0 + i: w2w[n][:, i, :] for n, (e0, count) in enumerate(W2_LOADS) for i in range(count)}
         w1s = held([P, H], U8, "w1s")
         w2s = held([P, N], U8, "w2s")
-        g1 = [held([P, 2 * C], F32, "g1%d" % a) for a in range(2)]
+        gate_rows = [held([P, C], F32, "gate_rows%d" % n) for n in range(2)]
+        g1 = held([P, E * C], F32, "g1")
         g2 = held([P, E * C], F32, "g2")
         raw = [held([P, PACK, H], F32, "raw%d" % k, raw_at(k)) for k in range(PASSES)]
-        text_out = [held([P, T], F32, "text_out%d" % b) for b in range(N_TILES)]
+        window_at = (None, raw_at(1), raw_at(2), raw_at(2) + T * 4)
+        text_out = [held([P, T], F32, "text_out%d" % b, window_at[b]) for b in range(N_TILES)]
         patch_out = [held([P, Q], F32, "patch_out%d" % b) for b in range(N_TILES)]
+
+        ident = held([P, P], F32, "ident")
 
         for plane in (xs, w1s):
             nc.gpsimd.memset(plane[:].bitcast(I32), 0)
+        for rows in gate_rows:
+            nc.gpsimd.memset(rows[:], 0.0)
         for plane in (w2s, zs):
             nc.vector.memset(plane[:].bitcast(I32), 0)
         for b in range(2):
@@ -107,40 +114,45 @@ def tile_moe_mmo_relu_kernel(
             rows = wz[e, s * P * PACK : (s + 1) * P * PACK, :]
             nc.sync.dma_start(out=raw[k][:], in_=rows.rearrange("(p j) c -> p j c", j=PACK))
 
-        def load_gate1(a):
-            nc.sync.dma_start(out=g1[a][:], in_=gate1[:, 2 * a * C : 2 * (a + 1) * C])
+        def load_gate(n, gate):
+            nc.sync.dma_start(out=gate_rows[n][0:E, :], in_=gate[0, :].rearrange("(e c) -> e c", e=E))
 
+        def spread_gate(n, gate):
+            turn = bank_tile([P, P], "gate_turn%d" % n, 4 + 2 * n)
+            nc.tensor.transpose(turn[:], gate_rows[n][:], ident[:])
+            columns = held([P, E], F32, "gate_columns%d" % n)
+            nc.scalar.copy(columns[:], turn[:, 0:E])
+            spread = bank_tile([P, E, C], "gate_spread%d" % n, 5 + 2 * n)
+            for e in range(E):
+                nc.tensor.transpose(spread[:, e, :], columns[:, e : e + 1].to_broadcast([P, P]), ident[:])
+            nc.scalar.copy(gate[:], spread[:].rearrange("p e c -> p (e c)"))
+
+        make_identity(nc, ident[:])
         load_words(xw, x_words[0])
         nc.sync.dma_start(offs_t[:], offs)
         load_scales(xs, x_scales)
         load_pair(w1w, w1_words, 0)
-        load_gate1(0)
+        load_gate(0, gate1)
         load_scales(w1s, w1_scales[:, 0])
         nc.sync.dma_start(offs2_t[:], offs2)
         load_words(zw[0], z_words[0])
         load_words(zw[1], z_words[1])
         load_w2(0)
         load_scales(w2s, w2_scales[:, 0])
-        load_wz(0)
-        load_scales(zs, z_scales)
-        load_wz(1)
-        nc.sync.dma_start(out=g2[:], in_=gate2)
-        load_wz(2)
-        load_wz(3)
-        load_wz(4)
+        load_gate(1, gate2)
+        for k in range(PASSES):
+            load_wz(k)
+            if k == 0:
+                load_scales(zs, z_scales)
         load_w2(1)
-        load_wz(5)
-        load_wz(6)
-        load_wz(7)
-        load_w2(2)
         load_pair(w1w, w1_words, 1)
-        load_gate1(1)
+        load_w2(2)
 
         xg = [held([P, 2 * C], U32, "xg%d" % a) for a in range(2)]
         xgs = [held([P, 2 * C], U8, "xgs%d" % a) for a in range(2)]
         zg = [held([P, E * C], U32, "zg%d" % s) for s in range(Z_PASSES)]
         zgs = held([P, E * C], U8, "zgs")
-        w1g = [held([P, 2, PACK, P], U32, "w1g0"), held([P, 2, PACK, P], U32, "w1g1", grouped_at(PASSES - 1))]
+        w1g = [held([P, 2, PACK, P], U32, "w1g0")]
         w1gs = held([P, PACK, P], U8, "w1gs")
 
         def gather_text(a):
@@ -174,6 +186,31 @@ def tile_moe_mmo_relu_kernel(
                         rhs_scale=xgs[a][:, slots], start=True, stop=True,
                     )
                 nc.scalar.activation(hidden[:, slots, :], acc[:].rearrange("p (t c) -> p c t", t=PACK), RELU)
+            return hidden
+
+        def text_rows(a, offset):
+            turn = bank_tile([P, 2, 2, C], "turn", 0)
+            for i in range(2):
+                e = 2 * a + i
+                slots = slice(i * C, (i + 1) * C)
+                acc = bank_tile([P, H], "acc_t%d" % e, 6 + i)
+                nc.tensor.matmul_mx(
+                    out=acc[:], lhsT=xg[a][:, slots].bitcast(FP8X4), lhsT_scale=xgs[a][:, slots],
+                    rhs=w1w[a][:, i, :].bitcast(FP8X4), rhs_scale=w1s[4 * e :, :], start=True, stop=True,
+                )
+                rows = held([P, H], BF16, "rows%d" % e, offset + i * H * 2)
+                nc.vector.tensor_scalar_max(rows[:], acc[:], 0.0)
+                pairs = rows[:].bitcast(F32)
+                for u in range(2):
+                    nc.tensor.transpose(turn[:, i, u, :], pairs[:, u : H // 2 : 2], ident[:])
+            return turn
+
+        def leave_turned(a, turn):
+            hidden = held([P, 2 * C, PACK], BF16, "hidden_t%d" % a)
+            nc.vector.tensor_copy(
+                hidden[:].rearrange("p c t -> p (c t)").bitcast(F32).rearrange("p (i c u) -> p i c u", i=2, u=2),
+                turn[:].rearrange("p i u c -> p i c u"),
+            )
             return hidden
 
         def patch_hidden(e):
@@ -231,7 +268,7 @@ def tile_moe_mmo_relu_kernel(
 
         def gated_text(a, banks, b0, b1, offset=None, res=None):
             i = b0 // 2
-            res = gated(banks[i], b0 - 2 * i, b1 - 2 * i, g1[a][:], "t%d%d" % (a, i), offset, res)
+            res = gated(banks[i], b0 - 2 * i, b1 - 2 * i, g1[:, 2 * a * C : 2 * (a + 1) * C], "t%d%d" % (a, i), offset, res)
             return {2 * i + b: v for b, v in res.items()}
 
         def gated_patches(e, bank, b0, b1, offset=None):
@@ -246,6 +283,10 @@ def tile_moe_mmo_relu_kernel(
         def put_text(a, res, blocks, on_scalar=True):
             for b in blocks:
                 scatter(text_out[b], offs_t[:, 2 * a * COLS : 2 * (a + 1) * COLS], res[b], on_scalar)
+
+        def put_text_half(e, res, b, on_scalar):
+            i = e % 2
+            scatter(text_out[b], offs_t[:, e * COLS : (e + 1) * COLS], res[b][:, i * C : (i + 1) * C], on_scalar)
 
         def put_patches(e, res, blocks, on_scalar=True):
             for b in blocks:
@@ -262,7 +303,7 @@ def tile_moe_mmo_relu_kernel(
             nc.vector.tensor_copy(dst[:, on_scalar:], src[:, on_scalar:])
 
         def quantise_wz(k):
-            codes = held([P, H], U32, "wcodes%d" % k)
+            codes = held([P, H], U32, "wcodes%d" % k, grouped_at(PASSES) if k == PASSES - 1 else None)
             scales = held([P, H], U8, "wscales%d" % k)
             nc.vector.quantize_mx(
                 out=codes[:].bitcast(FP8X4), scales=scales[:], in_=grouped[k][:].rearrange("p t m j -> p (t m j)")
@@ -276,6 +317,7 @@ def tile_moe_mmo_relu_kernel(
             nc.sync.dma_start(out=out[b * P : (b + 1) * P, T : T + Q], in_=patch_out[b][:])
 
         gather_text(0)
+        spread_gate(0, g1)
         regroup_w1(0, True)
         nc.vector.tensor_copy(w1gs[:].rearrange("p t m -> p m t"), w1s[:].rearrange("p (m t) -> p m t", t=PACK))
         gather_text(1)
@@ -283,12 +325,15 @@ def tile_moe_mmo_relu_kernel(
         for s in range(Z_PASSES):
             nc.vector.tensor_copy(zg[s][:], zw[s][:].bitcast(U32).indirect(offs2_t[:]))
         banks = second_product(quantise_hidden(hidden, "t0"), 0, 2, "t0", 2)
-        put_text(0, gated_text(0, banks, 0, 1), (0,))
+        spread_gate(1, g2)
+        first_sums = gated_text(0, banks, 0, 2)
+        put_text(0, first_sums, (0,))
+        first_sums.update(gated_text(0, banks, 2, 4))
         cast_wz(0)
         nc.vector.tensor_copy(zgs[:], zs[:].indirect(offs2_t[:]))
         quantise_wz(0)
         cast_wz(1, P // 2)
-        put_text(0, gated_text(0, banks, 1, 2, None, raw[1][:, 0:1, 0 : 2 * C]), (1,))
+        put_text(0, first_sums, (1,))
         quantise_wz(1)
         hidden = patch_hidden(0)
         sums = {}
@@ -296,7 +341,7 @@ def tile_moe_mmo_relu_kernel(
             k = Z_PASSES * e
             cast_wz(k)
             if e == 1:
-                put_text(0, gated_text(0, banks, 2, 4, raw_at(k)), (2, 3))
+                put_text(0, first_sums, (2, 3))
             else:
                 put_patches(e - 2, gated_patches(e - 2, sums[e - 2], 1, 4, raw_at(k)), (1, 2, 3))
             quantise_wz(k)
@@ -306,21 +351,21 @@ def tile_moe_mmo_relu_kernel(
             put_patches(e - 1, gated_patches(e - 1, sums[e - 1], 0, count), range(count))
             quantise_wz(k + 1)
             hidden = patch_hidden(e)
-        rest = gated_patches(2, sums[2], 2, 4, raw_at(PASSES - 1))
-        regroup_w1(1, False)
+        turn = text_rows(1, raw_at(PASSES - 1))
+        put_patches(2, gated_patches(2, sums[2], 2, 4, grouped_at(PASSES)), (2, 3))
         last = second_product(quantise_hidden(hidden, "p3"), 3, 1, "p3", 5)[0]
-        put_patches(2, rest, (3,), False)
-        hidden = text_hidden(1, None)
+        hidden = leave_turned(1, turn)
         put_patches(3, gated_patches(3, last, 0, 2), (0, 1))
         banks = second_product(quantise_hidden(hidden, "t1"), 2, 2, "t1", 2)
         res = gated_patches(3, last, 2, 4)
-        put_patches(3, res, (2,), False)
-        put_patches(2, rest, (2,))
         early = gated_text(1, banks, 0, 2)
-        put_patches(3, res, (3,), False)
+        put_patches(3, res, (3, 2), False)
         put_text(1, early, (0, 1))
-        put_text(1, gated_text(1, banks, 2, 4), (3, 2), False)
-        for b in (0, 1, 3, 2):
-            store_patches(b)
+        late = gated_text(1, banks, 2, 4)
+        put_text_half(3, late, 2, False)
+        put_text(1, late, (3,), False)
+        put_text_half(2, late, 2, True)
         for b in (0, 3, 1, 2):
+            store_patches(b)
+        for b in (0, 1, 3, 2):
             store_text(b)

@@ -271,8 +271,8 @@ def tile_moe_mmo_relu_kernel(
             res = gated(banks[i], b0 - 2 * i, b1 - 2 * i, g1[:, 2 * a * C : 2 * (a + 1) * C], "t%d%d" % (a, i), offset, res)
             return {2 * i + b: v for b, v in res.items()}
 
-        def gated_patches(e, bank, b0, b1, offset=None):
-            return gated(bank, b0, b1, g2[:, e * C : (e + 1) * C], "p%d" % e, offset)
+        def gated_patches(e, bank, b0, b1, offset=None, res=None):
+            return gated(bank, b0, b1, g2[:, e * C : (e + 1) * C], "p%d" % e, offset, res)
 
         def scatter(window, offsets, values, on_scalar):
             if on_scalar:
@@ -294,13 +294,15 @@ def tile_moe_mmo_relu_kernel(
 
         grouped, quantised = {}, {}
 
-        def cast_wz(k, on_scalar=0):
+        def cast_wz(k, on_scalar=0, halves=False):
             grouped[k] = held([P, PACK, P, PACK], BF16, "grouped%d" % k, grouped_at(k))
             dst = grouped[k][:].rearrange("p t m j -> p m j t")
             src = raw[k][:].rearrange("p j (m t) -> p m j t", t=PACK)
             if on_scalar:
-                nc.scalar.copy(dst[:, :on_scalar], src[:, :on_scalar])
-            nc.vector.tensor_copy(dst[:, on_scalar:], src[:, on_scalar:])
+                nc.scalar.copy(dst[:, P - on_scalar :], src[:, P - on_scalar :])
+            cuts = (0, (P - on_scalar) // 2, P - on_scalar) if halves else (0, P - on_scalar)
+            for m0, m1 in zip(cuts, cuts[1:]):
+                nc.vector.tensor_copy(dst[:, m0:m1], src[:, m0:m1])
 
         def quantise_wz(k):
             codes = held([P, H], U32, "wcodes%d" % k, grouped_at(PASSES) if k == PASSES - 1 else None)
@@ -332,20 +334,23 @@ def tile_moe_mmo_relu_kernel(
         cast_wz(0)
         nc.vector.tensor_copy(zgs[:], zs[:].indirect(offs2_t[:]))
         quantise_wz(0)
-        cast_wz(1, P // 2)
+        cast_wz(1, 3 * P // 4)
         put_text(0, first_sums, (1,))
         quantise_wz(1)
         hidden = patch_hidden(0)
         sums = {}
         for e in range(1, E):
             k = Z_PASSES * e
-            cast_wz(k)
+            cast_wz(k, 0, e > 1)
             if e == 1:
                 put_text(0, first_sums, (2, 3))
+                codes = quantise_hidden(hidden, "p0")
             else:
-                put_patches(e - 2, gated_patches(e - 2, sums[e - 2], 1, 4, raw_at(k)), (1, 2, 3))
+                put_patches(e - 2, gated_patches(e - 2, sums[e - 2], 1, 4, None, raw[k][:, 0:3, 0:C]), (1, 2, 3))
             quantise_wz(k)
-            sums[e - 1] = second_product(quantise_hidden(hidden, "p%d" % (e - 1)), e - 1, 1, "p%d" % (e - 1), 4 + (e - 1) % 2)[0]
+            if e > 1:
+                codes = quantise_hidden(hidden, "p%d" % (e - 1))
+            sums[e - 1] = second_product(codes, e - 1, 1, "p%d" % (e - 1), 4 + (e - 1) % 2)[0]
             cast_wz(k + 1)
             count = 2 if e == E - 1 else 1
             put_patches(e - 1, gated_patches(e - 1, sums[e - 1], 0, count), range(count))

@@ -66,8 +66,7 @@ def tile_moe_mmo_relu_kernel(
         w2_of = {e0 + i: w2w[n][:, i, :] for n, (e0, count) in enumerate(W2_LOADS) for i in range(count)}
         w1s = held([P, H], U8, "w1s")
         w2s = held([P, N], U8, "w2s")
-        gate_rows = [held([P, C], F32, "gate_rows%d" % n) for n in range(2)]
-        g1 = held([P, E * C], F32, "g1")
+        g1 = [held([P, 2 * C], F32, "g1%d" % a) for a in range(2)]
         g2 = held([P, E * C], F32, "g2")
         raw = [held([P, PACK, H], F32, "raw%d" % k, raw_at(k)) for k in range(PASSES)]
         window_at = (None, raw_at(1), raw_at(2), raw_at(2) + T * 4)
@@ -78,8 +77,6 @@ def tile_moe_mmo_relu_kernel(
 
         for plane in (xs, w1s):
             nc.gpsimd.memset(plane[:].bitcast(I32), 0)
-        for rows in gate_rows:
-            nc.gpsimd.memset(rows[:], 0.0)
         for plane in (w2s, zs):
             nc.vector.memset(plane[:].bitcast(I32), 0)
         for b in range(2):
@@ -114,39 +111,31 @@ def tile_moe_mmo_relu_kernel(
             rows = wz[e, s * P * PACK : (s + 1) * P * PACK, :]
             nc.sync.dma_start(out=raw[k][:], in_=rows.rearrange("(p j) c -> p j c", j=PACK))
 
-        def load_gate(n, gate):
-            nc.sync.dma_start(out=gate_rows[n][0:E, :], in_=gate[0, :].rearrange("(e c) -> e c", e=E))
-
-        def spread_gate(n, gate):
-            turn = bank_tile([P, P], "gate_turn%d" % n, 4 + 2 * n)
-            nc.tensor.transpose(turn[:], gate_rows[n][:], ident[:])
-            columns = held([P, E], F32, "gate_columns%d" % n)
-            nc.scalar.copy(columns[:], turn[:, 0:E])
-            spread = bank_tile([P, E, C], "gate_spread%d" % n, 5 + 2 * n)
-            for e in range(E):
-                nc.tensor.transpose(spread[:, e, :], columns[:, e : e + 1].to_broadcast([P, P]), ident[:])
-            nc.scalar.copy(gate[:], spread[:].rearrange("p e c -> p (e c)"))
+        def load_gate1(a):
+            nc.sync.dma_start(out=g1[a][:], in_=gate1[:, 2 * a * C : 2 * (a + 1) * C])
 
         make_identity(nc, ident[:])
         load_words(xw, x_words[0])
         nc.sync.dma_start(offs_t[:], offs)
         load_scales(xs, x_scales)
         load_pair(w1w, w1_words, 0)
-        load_gate(0, gate1)
+        load_words(zw[0], z_words[0])
         load_scales(w1s, w1_scales[:, 0])
         nc.sync.dma_start(offs2_t[:], offs2)
-        load_words(zw[0], z_words[0])
         load_words(zw[1], z_words[1])
         load_w2(0)
         load_scales(w2s, w2_scales[:, 0])
-        load_gate(1, gate2)
+        load_gate1(0)
         for k in range(PASSES):
             load_wz(k)
             if k == 0:
                 load_scales(zs, z_scales)
+            if k == 1:
+                nc.sync.dma_start(out=g2[:], in_=gate2)
         load_w2(1)
         load_pair(w1w, w1_words, 1)
         load_w2(2)
+        load_gate1(1)
 
         xg = [held([P, 2 * C], U32, "xg%d" % a) for a in range(2)]
         xgs = [held([P, 2 * C], U8, "xgs%d" % a) for a in range(2)]
@@ -188,22 +177,22 @@ def tile_moe_mmo_relu_kernel(
                 nc.scalar.activation(hidden[:, slots, :], acc[:].rearrange("p (t c) -> p c t", t=PACK), RELU)
             return hidden
 
-        def text_rows(a, offset):
-            turn = bank_tile([P, 2, 2, C], "turn", 0)
-            for i in range(2):
-                e = 2 * a + i
-                slots = slice(i * C, (i + 1) * C)
-                acc = bank_tile([P, H], "acc_t%d" % e, 6 + i)
-                nc.tensor.matmul_mx(
-                    out=acc[:], lhsT=xg[a][:, slots].bitcast(FP8X4), lhsT_scale=xgs[a][:, slots],
-                    rhs=w1w[a][:, i, :].bitcast(FP8X4), rhs_scale=w1s[4 * e :, :], start=True, stop=True,
-                )
-                rows = held([P, H], BF16, "rows%d" % e, offset + i * H * 2)
+        def text_rows(e, turn, offset, on_scalar):
+            a, i = divmod(e, 2)
+            slots = slice(i * C, (i + 1) * C)
+            acc = bank_tile([P, H], "acc_t%d" % e, 6 + i)
+            nc.tensor.matmul_mx(
+                out=acc[:], lhsT=xg[a][:, slots].bitcast(FP8X4), lhsT_scale=xgs[a][:, slots],
+                rhs=w1w[a][:, i, :].bitcast(FP8X4), rhs_scale=w1s[4 * e :, :], start=True, stop=True,
+            )
+            rows = held([P, H], BF16, "rows%d" % e, offset)
+            if on_scalar:
+                nc.scalar.activation(rows[:], acc[:], RELU)
+            else:
                 nc.vector.tensor_scalar_max(rows[:], acc[:], 0.0)
-                pairs = rows[:].bitcast(F32)
-                for u in range(2):
-                    nc.tensor.transpose(turn[:, i, u, :], pairs[:, u : H // 2 : 2], ident[:])
-            return turn
+            pairs = rows[:].bitcast(F32)
+            for u in range(2):
+                nc.tensor.transpose(turn[:, i, u, :], pairs[:, u : H // 2 : 2], ident[:])
 
         def leave_turned(a, turn):
             hidden = held([P, 2 * C, PACK], BF16, "hidden_t%d" % a)
@@ -213,7 +202,7 @@ def tile_moe_mmo_relu_kernel(
             )
             return hidden
 
-        def patch_hidden(e):
+        def patch_hidden(e, offset=None):
             slots = slice(e * C, (e + 1) * C)
             acc = bank_tile([P, H], "acc_p%d" % e, e % 2)
             for s in range(Z_PASSES):
@@ -225,7 +214,7 @@ def tile_moe_mmo_relu_kernel(
                         rhs=zg[s][:, slots].bitcast(FP8X4), rhs_scale=zgs[4 * s :, slots],
                         start=(s == 0 and t == 0), stop=(s == Z_PASSES - 1 and t == PACK - 1),
                     )
-            hidden = held([P, C, PACK], BF16, "hidden_p%d" % e)
+            hidden = held([P, C, PACK], BF16, "hidden_p%d" % e, offset)
             nc.scalar.activation(hidden[:], acc[:].rearrange("p (t c) -> p c t", t=PACK), RELU)
             return hidden
 
@@ -268,7 +257,7 @@ def tile_moe_mmo_relu_kernel(
 
         def gated_text(a, banks, b0, b1, offset=None, res=None):
             i = b0 // 2
-            res = gated(banks[i], b0 - 2 * i, b1 - 2 * i, g1[:, 2 * a * C : 2 * (a + 1) * C], "t%d%d" % (a, i), offset, res)
+            res = gated(banks[i], b0 - 2 * i, b1 - 2 * i, g1[a][:], "t%d%d" % (a, i), offset, res)
             return {2 * i + b: v for b, v in res.items()}
 
         def gated_patches(e, bank, b0, b1, offset=None, res=None):
@@ -304,12 +293,23 @@ def tile_moe_mmo_relu_kernel(
             for m0, m1 in zip(cuts, cuts[1:]):
                 nc.vector.tensor_copy(dst[:, m0:m1], src[:, m0:m1])
 
-        def quantise_wz(k):
+        def cast_last(k):
+            grouped[k] = held([P, PACK, P, PACK], BF16, "grouped%d" % k, grouped_at(k))
+            dst = grouped[k][:].rearrange("p t m j -> p m j t")
+            src = raw[k][:].rearrange("p j (m t) -> p m j t", t=PACK)
+            for t in (0, 2):
+                nc.vector.tensor_copy(dst[:, :, :, t : t + 2], src[:, :, :, t : t + 2])
+
+        def quantise_wz(k, parts=1):
             codes = held([P, H], U32, "wcodes%d" % k, grouped_at(PASSES) if k == PASSES - 1 else None)
             scales = held([P, H], U8, "wscales%d" % k)
-            nc.vector.quantize_mx(
-                out=codes[:].bitcast(FP8X4), scales=scales[:], in_=grouped[k][:].rearrange("p t m j -> p (t m j)")
-            )
+            width = H // parts
+            values = grouped[k][:].rearrange("p t m j -> p (t m j)")
+            for c in range(0, H, width):
+                nc.vector.quantize_mx(
+                    out=codes[:, c : c + width].bitcast(FP8X4), scales=scales[:, c : c + width],
+                    in_=values[:, PACK * c : PACK * (c + width)],
+                )
             quantised[k] = codes, scales
 
         def store_text(b):
@@ -319,15 +319,13 @@ def tile_moe_mmo_relu_kernel(
             nc.sync.dma_start(out=out[b * P : (b + 1) * P, T : T + Q], in_=patch_out[b][:])
 
         gather_text(0)
-        spread_gate(0, g1)
         regroup_w1(0, True)
         nc.vector.tensor_copy(w1gs[:].rearrange("p t m -> p m t"), w1s[:].rearrange("p (m t) -> p m t", t=PACK))
         gather_text(1)
         hidden = text_hidden(0, None)
         for s in range(Z_PASSES):
             nc.vector.tensor_copy(zg[s][:], zw[s][:].bitcast(U32).indirect(offs2_t[:]))
-        banks = second_product(quantise_hidden(hidden, "t0"), 0, 2, "t0", 2)
-        spread_gate(1, g2)
+        banks = second_product(quantise_hidden(hidden, "t0", grouped_at(0)), 0, 2, "t0", 2)
         first_sums = gated_text(0, banks, 0, 2)
         put_text(0, first_sums, (0,))
         first_sums.update(gated_text(0, banks, 2, 4))
@@ -351,26 +349,33 @@ def tile_moe_mmo_relu_kernel(
             if e > 1:
                 codes = quantise_hidden(hidden, "p%d" % (e - 1))
             sums[e - 1] = second_product(codes, e - 1, 1, "p%d" % (e - 1), 4 + (e - 1) % 2)[0]
-            cast_wz(k + 1)
-            count = 2 if e == E - 1 else 1
-            put_patches(e - 1, gated_patches(e - 1, sums[e - 1], 0, count), range(count))
-            quantise_wz(k + 1)
+            if e < E - 1:
+                cast_wz(k + 1)
+            else:
+                cast_last(k + 1)
+            put_patches(e - 1, gated_patches(e - 1, sums[e - 1], 0, 1), (0,))
+            quantise_wz(k + 1, 1 if e < E - 1 else 2)
             hidden = patch_hidden(e)
-        turn = text_rows(1, raw_at(PASSES - 1))
-        put_patches(2, gated_patches(2, sums[2], 2, 4, grouped_at(PASSES)), (2, 3))
+        turn = bank_tile([P, 2, 2, C], "turn", 0)
+        text_rows(2, turn, raw_at(PASSES - 1), False)
+        text_rows(3, turn, grouped_at(PASSES) + 2 * C * 4, True)
+        rest = gated_patches(2, sums[2], 1, 3, grouped_at(PASSES))
+        put_patches(2, rest, (1,))
         last = second_product(quantise_hidden(hidden, "p3"), 3, 1, "p3", 5)[0]
+        put_patches(2, rest, (2,), False)
+        put_patches(3, gated_patches(3, last, 0, 3), (0, 1, 2))
         hidden = leave_turned(1, turn)
-        put_patches(3, gated_patches(3, last, 0, 2), (0, 1))
-        banks = second_product(quantise_hidden(hidden, "t1"), 2, 2, "t1", 2)
-        res = gated_patches(3, last, 2, 4)
-        early = gated_text(1, banks, 0, 2)
-        put_patches(3, res, (3, 2), False)
-        put_text(1, early, (0, 1))
+        res = gated_patches(3, last, 3, 4)
+        banks = second_product(quantise_hidden(hidden, "t1", grouped_at(1)), 2, 2, "t1", 2)
+        put_patches(3, res, (3,), False)
+        put_text(1, gated_text(1, banks, 0, 2), (0, 1))
+        rest = gated_patches(2, sums[2], 3, 4, grouped_at(1))
         late = gated_text(1, banks, 2, 4)
+        put_patches(2, rest, (3,), False)
         put_text_half(3, late, 2, False)
         put_text(1, late, (3,), False)
         put_text_half(2, late, 2, True)
-        for b in (0, 3, 1, 2):
+        for b in (0, 1, 2, 3):
             store_patches(b)
         for b in (0, 1, 3, 2):
             store_text(b)

@@ -69,7 +69,7 @@ def tile_moe_mmo_relu_kernel(
         g1 = [held([P, 2 * C], F32, "g1%d" % a) for a in range(2)]
         g2 = held([P, E * C], F32, "g2")
         raw = [held([P, PACK, H], F32, "raw%d" % k, raw_at(k)) for k in range(PASSES)]
-        window_at = (None, raw_at(1), raw_at(2), raw_at(2) + T * 4)
+        window_at = (None, None, raw_at(1), raw_at(2))
         text_out = [held([P, T], F32, "text_out%d" % b, window_at[b]) for b in range(N_TILES)]
         patch_out = [held([P, Q], F32, "patch_out%d" % b) for b in range(N_TILES)]
 
@@ -327,13 +327,13 @@ def tile_moe_mmo_relu_kernel(
             nc.vector.tensor_copy(zg[s][:], zw[s][:].bitcast(U32).indirect(offs2_t[:]))
         banks = second_product(quantise_hidden(hidden, "t0", grouped_at(0)), 0, 2, "t0", 2)
         first_sums = gated_text(0, banks, 0, 2)
-        put_text(0, first_sums, (0,))
+        put_text(0, first_sums, (0, 1))
         first_sums.update(gated_text(0, banks, 2, 4))
         cast_wz(0)
         nc.vector.tensor_copy(zgs[:], zs[:].indirect(offs2_t[:]))
         quantise_wz(0)
-        cast_wz(1, 3 * P // 4)
-        put_text(0, first_sums, (1,))
+        cast_wz(1)
+        put_text(0, first_sums, (2,))
         quantise_wz(1)
         hidden = patch_hidden(0)
         sums = {}
@@ -341,7 +341,7 @@ def tile_moe_mmo_relu_kernel(
             k = Z_PASSES * e
             cast_wz(k, 0, e > 1)
             if e == 1:
-                put_text(0, first_sums, (2, 3))
+                put_text(0, first_sums, (3,))
                 codes = quantise_hidden(hidden, "p0")
             else:
                 put_patches(e - 2, gated_patches(e - 2, sums[e - 2], 1, 4, None, raw[k][:, 0:3, 0:C]), (1, 2, 3))

@@ -69,7 +69,7 @@ def tile_moe_mmo_relu_kernel(
         g1 = [held([P, 2 * C], F32, "g1%d" % a) for a in range(2)]
         g2 = held([P, E * C], F32, "g2")
         raw = [held([P, PACK, H], F32, "raw%d" % k, raw_at(k)) for k in range(PASSES)]
-        window_at = (None, None, raw_at(1), raw_at(2))
+        window_at = (None, None, None, grouped_at(2))
         text_out = [held([P, T], F32, "text_out%d" % b, window_at[b]) for b in range(N_TILES)]
         patch_out = [held([P, Q], F32, "patch_out%d" % b) for b in range(N_TILES)]
 
@@ -247,6 +247,21 @@ def tile_moe_mmo_relu_kernel(
                 banks.append(acc)
             return banks
 
+        def block_sums(operand, e0, blocks, name, bank):
+            codes, scales = operand
+            width = codes.shape[1]
+            acc = bank_tile([P, len(blocks), width], "sums" + name, bank)
+            for i in range(width // C):
+                slots = slice(i * C, (i + 1) * C)
+                for n, b in enumerate(blocks):
+                    cols = slice(b * P, (b + 1) * P)
+                    nc.tensor.matmul_mx(
+                        out=acc[:, n, slots], lhsT=w2_of[e0 + i][:, cols].bitcast(FP8X4),
+                        lhsT_scale=w2s[4 * (e0 + i) :, cols], rhs=codes[:, slots].bitcast(FP8X4),
+                        rhs_scale=scales[:, slots], start=True, stop=True,
+                    )
+            return acc
+
         def gated(bank, b0, b1, gate, name, offset=None, res=None):
             shape = [P, b1 - b0, bank.shape[2]]
             if res is None:
@@ -273,9 +288,9 @@ def tile_moe_mmo_relu_kernel(
             for b in blocks:
                 scatter(text_out[b], offs_t[:, 2 * a * COLS : 2 * (a + 1) * COLS], res[b], on_scalar)
 
-        def put_text_half(e, res, b, on_scalar):
-            i = e % 2
-            scatter(text_out[b], offs_t[:, e * COLS : (e + 1) * COLS], res[b][:, i * C : (i + 1) * C], on_scalar)
+        def put_text_part(a, res, b, c0, c1, on_scalar):
+            first = 2 * a * COLS
+            scatter(text_out[b], offs_t[:, first + c0 : first + c1], res[b][:, 16 * c0 : 16 * c1], on_scalar)
 
         def put_patches(e, res, blocks, on_scalar=True):
             for b in blocks:
@@ -325,29 +340,29 @@ def tile_moe_mmo_relu_kernel(
         hidden = text_hidden(0, None)
         for s in range(Z_PASSES):
             nc.vector.tensor_copy(zg[s][:], zw[s][:].bitcast(U32).indirect(offs2_t[:]))
-        banks = second_product(quantise_hidden(hidden, "t0", grouped_at(0)), 0, 2, "t0", 2)
-        first_sums = gated_text(0, banks, 0, 2)
-        put_text(0, first_sums, (0, 1))
-        first_sums.update(gated_text(0, banks, 2, 4))
-        cast_wz(0)
-        nc.vector.tensor_copy(zgs[:], zs[:].indirect(offs2_t[:]))
-        quantise_wz(0)
-        cast_wz(1)
+        codes = quantise_hidden(hidden, "t0", grouped_at(0))
+        for b in range(2):
+            put_text(0, {b: gated(block_sums(codes, 0, (b,), "t0%d" % b, 2 + b), 0, 1, g1[0][:], "t0%d" % b)[0]}, (b,))
+        res = gated(block_sums(codes, 0, (2, 3), "t02", 4), 0, 2, g1[0][:], "t02")
+        first_sums = {2: res[0], 3: res[1]}
         put_text(0, first_sums, (2,))
-        quantise_wz(1)
-        hidden = patch_hidden(0)
+        cast_last(0)
+        nc.vector.tensor_copy(zgs[:], zs[:].indirect(offs2_t[:]))
+        quantise_wz(0, 2)
+        cast_last(1)
+        quantise_wz(1, 2)
         sums = {}
         for e in range(1, E):
             k = Z_PASSES * e
-            cast_wz(k, 0, e > 1)
+            cast_wz(k, 3 * P // 8 if e == 1 else 0, e > 1)
             if e == 1:
-                put_text(0, first_sums, (3,))
-                codes = quantise_hidden(hidden, "p0")
+                hidden = patch_hidden(0, raw_at(k))
             else:
                 put_patches(e - 2, gated_patches(e - 2, sums[e - 2], 1, 4, None, raw[k][:, 0:3, 0:C]), (1, 2, 3))
             quantise_wz(k)
-            if e > 1:
-                codes = quantise_hidden(hidden, "p%d" % (e - 1))
+            if e == 1:
+                put_text(0, first_sums, (3,))
+            codes = quantise_hidden(hidden, "p%d" % (e - 1))
             sums[e - 1] = second_product(codes, e - 1, 1, "p%d" % (e - 1), 4 + (e - 1) % 2)[0]
             if e < E - 1:
                 cast_wz(k + 1)
@@ -361,20 +376,23 @@ def tile_moe_mmo_relu_kernel(
         text_rows(3, turn, grouped_at(PASSES) + 2 * C * 4, True)
         rest = gated_patches(2, sums[2], 1, 3, grouped_at(PASSES))
         put_patches(2, rest, (1,))
-        last = second_product(quantise_hidden(hidden, "p3"), 3, 1, "p3", 5)[0]
+        codes = quantise_hidden(hidden, "p3")
+        lead = block_sums(codes, 3, (0,), "p3a", 1)
+        last = block_sums(codes, 3, (1, 2, 3), "p3b", 5)
         put_patches(2, rest, (2,), False)
-        put_patches(3, gated_patches(3, last, 0, 3), (0, 1, 2))
+        put_patches(3, gated_patches(3, lead, 0, 1), (0,))
+        put_patches(3, {b + 1: v for b, v in gated(last, 0, 2, g2[:, 3 * C :], "p3b").items()}, (1, 2))
         hidden = leave_turned(1, turn)
-        res = gated_patches(3, last, 3, 4)
+        res = {3: gated(last, 2, 3, g2[:, 3 * C :], "p3b", grouped_at(PASSES) + 2 * C * 4)[2]}
         banks = second_product(quantise_hidden(hidden, "t1", grouped_at(1)), 2, 2, "t1", 2)
         put_patches(3, res, (3,), False)
         put_text(1, gated_text(1, banks, 0, 2), (0, 1))
         rest = gated_patches(2, sums[2], 3, 4, grouped_at(1))
         late = gated_text(1, banks, 2, 4)
         put_patches(2, rest, (3,), False)
-        put_text_half(3, late, 2, False)
+        put_text_part(1, late, 2, COLS, 2 * COLS, False)
         put_text(1, late, (3,), False)
-        put_text_half(2, late, 2, True)
+        put_text_part(1, late, 2, 0, COLS, True)
         for b in (0, 1, 2, 3):
             store_patches(b)
         for b in (0, 1, 3, 2):

@@ -68,15 +68,16 @@ def tile_moe_mmo_relu_kernel(
         w2s = held([P, N], U8, "w2s")
         g1 = [held([P, 2 * C], F32, "g1%d" % a) for a in range(2)]
         g2 = held([P, E * C], F32, "g2")
+        gate_rows = held([P, C], F32, "gate_rows")
         raw = [held([P, PACK, H], F32, "raw%d" % k, raw_at(k)) for k in range(PASSES)]
-        window_at = (None, None, None, grouped_at(2))
-        text_out = [held([P, T], F32, "text_out%d" % b, window_at[b]) for b in range(N_TILES)]
+        text_out = [held([P, T], F32, "text_out%d" % b) for b in range(N_TILES)]
         patch_out = [held([P, Q], F32, "patch_out%d" % b) for b in range(N_TILES)]
 
         ident = held([P, P], F32, "ident")
 
         for plane in (xs, w1s):
             nc.gpsimd.memset(plane[:].bitcast(I32), 0)
+        nc.gpsimd.memset(gate_rows[:], 0.0)
         for plane in (w2s, zs):
             nc.vector.memset(plane[:].bitcast(I32), 0)
         for b in range(2):
@@ -114,7 +115,18 @@ def tile_moe_mmo_relu_kernel(
         def load_gate1(a):
             nc.sync.dma_start(out=g1[a][:], in_=gate1[:, 2 * a * C : 2 * (a + 1) * C])
 
+        def spread_gate2():
+            turn = bank_tile([P, P], "gate_turn", 5)
+            nc.tensor.transpose(turn[:], gate_rows[:], ident[:])
+            columns = held([P, E], F32, "gate_columns")
+            nc.scalar.copy(columns[:], turn[:, 0:E])
+            spread = bank_tile([P, E, C], "gate_spread", 0)
+            for e in range(E):
+                nc.tensor.transpose(spread[:, e, :], columns[:, e : e + 1].to_broadcast([P, P]), ident[:])
+            nc.scalar.copy(g2[:], spread[:].rearrange("p e c -> p (e c)"))
+
         make_identity(nc, ident[:])
+        nc.gpsimd.dma_start(out=gate_rows[0:E, :], in_=gate2[0, :].rearrange("(e c) -> e c", e=E))
         load_words(xw, x_words[0])
         nc.sync.dma_start(offs_t[:], offs)
         load_scales(xs, x_scales)
@@ -130,8 +142,6 @@ def tile_moe_mmo_relu_kernel(
             load_wz(k)
             if k == 0:
                 load_scales(zs, z_scales)
-            if k == 1:
-                nc.sync.dma_start(out=g2[:], in_=gate2)
         load_w2(1)
         load_pair(w1w, w1_words, 1)
         load_w2(2)
@@ -338,6 +348,7 @@ def tile_moe_mmo_relu_kernel(
         nc.vector.tensor_copy(w1gs[:].rearrange("p t m -> p m t"), w1s[:].rearrange("p (m t) -> p m t", t=PACK))
         gather_text(1)
         hidden = text_hidden(0, None)
+        spread_gate2()
         for s in range(Z_PASSES):
             nc.vector.tensor_copy(zg[s][:], zw[s][:].bitcast(U32).indirect(offs2_t[:]))
         codes = quantise_hidden(hidden, "t0", grouped_at(0))
@@ -345,30 +356,32 @@ def tile_moe_mmo_relu_kernel(
             put_text(0, {b: gated(block_sums(codes, 0, (b,), "t0%d" % b, 2 + b), 0, 1, g1[0][:], "t0%d" % b)[0]}, (b,))
         res = gated(block_sums(codes, 0, (2, 3), "t02", 4), 0, 2, g1[0][:], "t02")
         first_sums = {2: res[0], 3: res[1]}
-        put_text(0, first_sums, (2,))
+        put_text(0, first_sums, (2, 3))
         cast_last(0)
         nc.vector.tensor_copy(zgs[:], zs[:].indirect(offs2_t[:]))
         quantise_wz(0, 2)
         cast_last(1)
         quantise_wz(1, 2)
+        hidden = patch_hidden(0)
         sums = {}
         for e in range(1, E):
             k = Z_PASSES * e
-            cast_wz(k, 3 * P // 8 if e == 1 else 0, e > 1)
             if e == 1:
-                hidden = patch_hidden(0, raw_at(k))
+                cast_last(k)
+                quantise_wz(k, 2)
             else:
-                put_patches(e - 2, gated_patches(e - 2, sums[e - 2], 1, 4, None, raw[k][:, 0:3, 0:C]), (1, 2, 3))
-            quantise_wz(k)
-            if e == 1:
-                put_text(0, first_sums, (3,))
-            codes = quantise_hidden(hidden, "p%d" % (e - 1))
+                cast_wz(k, 0, True)
+                put_patches(e - 2, gated_patches(e - 2, sums[e - 2], 2, 4, None, raw[k][:, 0:2, 0:C]), (2, 3))
+                quantise_wz(k)
+            codes = quantise_hidden(hidden, "p%d" % (e - 1), grouped_at(k) if e == 1 else None)
             sums[e - 1] = second_product(codes, e - 1, 1, "p%d" % (e - 1), 4 + (e - 1) % 2)[0]
             if e < E - 1:
-                cast_wz(k + 1)
+                cast_wz(k + 1, P // 2 if e == 1 else 0, True)
             else:
                 cast_last(k + 1)
-            put_patches(e - 1, gated_patches(e - 1, sums[e - 1], 0, 1), (0,))
+            count = 2 if e < E - 1 else 1
+            lead = raw[k + 1][:, 0:count, 0:C] if e < E - 1 else None
+            put_patches(e - 1, gated_patches(e - 1, sums[e - 1], 0, count, None, lead), range(count))
             quantise_wz(k + 1, 1 if e < E - 1 else 2)
             hidden = patch_hidden(e)
         turn = bank_tile([P, 2, 2, C], "turn", 0)

from contextlib import ExitStack

import concourse.mybir as mybir
from concourse.masks import make_identity

K, L, T, Q, E, C = 512, 1024, 512, 1024, 4, 128
H, N = 512, 512
FLOPS = 2 * E * C * (K * H + L * H + 2 * H * N)

F32 = mybir.dt.float32
BF16 = mybir.dt.bfloat16
I32 = mybir.dt.int32
U32 = mybir.dt.uint32
U16 = mybir.dt.uint16
U8 = mybir.dt.uint8
FP8X4 = mybir.dt.float8_e4m3fn_x4
RELU = mybir.ActivationFunctionType.Relu
COPY = mybir.ActivationFunctionType.Copy
MULT = mybir.AluOpType.mult

P = 128
PACK = 4
QUADS = 4
Z_PASSES = L // (P * PACK)
N_TILES = N // P
COLS = C // 16
PASSES = E * Z_PASSES
RAW_BYTES = PACK * H * 4
BANK_BYTES = 2048
W2_LOADS = ((0, 2), (2, 1), (3, 1))


def tile_moe_mmo_relu_kernel(
    tc, x_words, x_scales, z_words, z_scales, w1_words, w1_scales, wz, w2_words, w2_scales,
    gate1, gate2, offs, offs2, out
):
    nc = tc.nc
    with ExitStack() as ctx:
        keep = ctx.enter_context(tc.tile_pool(name="keep", bufs=1))
        psum = ctx.enter_context(tc.psum_pool(name="psum", bufs=1))

        shared = ctx.enter_context(tc.tile_pool(name="shared", bufs=1))

        def held(shape, dtype, name, offset=None):
            if offset is None:
                return keep.tile(shape, dtype, name=name, align_bytes=64)
            return shared.tile(shape, dtype, name=name, offset=offset, align_bytes=64)

        def bank_tile(shape, name, bank):
            return psum.tile(shape, F32, name=name, offset=bank * BANK_BYTES)

        def raw_at(k):
            return k * RAW_BYTES

        def grouped_at(k):
            return PASSES * RAW_BYTES + E * C + k * RAW_BYTES // 2

        offs_t = held([P, E * COLS], U16, "offs_t")
        offs2_t = held([P, E * COLS], U16, "offs2_t")
        xw = held([P, T], I32, "xw")
        xs = held([P, T], U8, "xs")
        zw = [held([P, Q], I32, "zw%d" % s) for s in range(Z_PASSES)]
        zs = held([P, Q], U8, "zs")
        w1w = [held([P, 2, H], I32, "w1w%d" % a) for a in range(2)]
        w2w = [held([P, count, N], I32, "w2w%d" % e) for e, count in W2_LOADS]
        w2_of = {e0 + i: w2w[n][:, i, :] for n, (e0, count) in enumerate(W2_LOADS) for i in range(count)}
        w1s = held([P, H], U8, "w1s")
        w2s = held([P, N], U8, "w2s")
        g1 = [held([P, 2 * C], F32, "g1%d" % a) for a in range(2)]
        g2 = held([P, E * C], F32, "g2")
        gate_rows = held([P, C], F32, "gate_rows")
        raw = [held([P, PACK, H], F32, "raw%d" % k, raw_at(k)) for k in range(PASSES)]
        text_out = [held([P, T], F32, "text_out%d" % b) for b in range(N_TILES)]
        patch_out = [held([P, Q], F32, "patch_out%d" % b) for b in range(N_TILES)]

        ident = held([P, P], F32, "ident")

        for plane in (xs, w1s):
            nc.gpsimd.memset(plane[:].bitcast(I32), 0)
        nc.gpsimd.memset(gate_rows[:], 0.0)
        for plane in (w2s, zs):
            nc.vector.memset(plane[:].bitcast(I32), 0)
        for b in range(2):
            nc.vector.memset(patch_out[b][:], 0.0)
        for b in range(2, N_TILES):
            nc.scalar.activation(patch_out[b][:], patch_out[0][:], RELU)

        def load_scales(plane, rows):
            count = rows.shape[0]
            for q in range(QUADS):
                nc.sync.dma_start(
                    out=plane[32 * q : 32 * q + 4 * count, :].bitcast(I32),
                    in_=rows[:, 4 * q : 4 * q + 4, :].bitcast(I32),
                )

        def load_words(tile, words):
            nc.sync.dma_start(out=tile[:], in_=words.rearrange("p c d -> p (c d)").bitcast(I32))

        def load_pair(tiles, words, a):
            nc.sync.dma_start(
                out=tiles[a][:], in_=words[2 * a : 2 * a + 2, 0].rearrange("e p c d -> p e (c d)").bitcast(I32)
            )

        def load_w2(n):
            e0, count = W2_LOADS[n]
            nc.sync.dma_start(
                out=w2w[n][:], in_=w2_words[e0 : e0 + count, 0].rearrange("e p c d -> p e (c d)").bitcast(I32)
            )

        def load_wz(k):
            e, s = divmod(k, Z_PASSES)
            rows = wz[e, s * P * PACK : (s + 1) * P * PACK, :]
            nc.sync.dma_start(out=raw[k][:], in_=rows.rearrange("(p j) c -> p j c", j=PACK))

        def load_gate1(a):
            nc.sync.dma_start(out=g1[a][:], in_=gate1[:, 2 * a * C : 2 * (a + 1) * C])

        def spread_gate2():
            turn = bank_tile([P, P], "gate_turn", 5)
            nc.tensor.transpose(turn[:], gate_rows[:], ident[:])
            columns = held([P, E], F32, "gate_columns")
            nc.scalar.copy(columns[:], turn[:, 0:E])
            spread = bank_tile([P, E, C], "gate_spread", 0)
            for e in range(E):
                nc.tensor.transpose(spread[:, e, :], columns[:, e : e + 1].to_broadcast([P, P]), ident[:])
            nc.scalar.copy(g2[:], spread[:].rearrange("p e c -> p (e c)"))

        make_identity(nc, ident[:])
        nc.gpsimd.dma_start(out=gate_rows[0:E, :], in_=gate2[0, :].rearrange("(e c) -> e c", e=E))
        load_words(xw, x_words[0])
        nc.sync.dma_start(offs_t[:], offs)
        load_scales(xs, x_scales)
        load_pair(w1w, w1_words, 0)
        load_words(zw[0], z_words[0])
        load_scales(w1s, w1_scales[:, 0])
        nc.sync.dma_start(offs2_t[:], offs2)
        load_words(zw[1], z_words[1])
        load_w2(0)
        load_scales(w2s, w2_scales[:, 0])
        load_gate1(0)
        for k in range(PASSES):
            load_wz(k)
            if k == 0:
                load_scales(zs, z_scales)
        load_w2(1)
        load_pair(w1w, w1_words, 1)
        load_w2(2)
        load_gate1(1)

        xg = [held([P, 2 * C], U32, "xg%d" % a) for a in range(2)]
        xgs = [held([P, 2 * C], U8, "xgs%d" % a) for a in range(2)]
        zg = [held([P, E * C], U32, "zg%d" % s) for s in range(Z_PASSES)]
        zgs = held([P, E * C], U8, "zgs")
        w1g = [held([P, 2, PACK, P], U32, "w1g0")]
        w1gs = held([P, PACK, P], U8, "w1gs")

        def gather_text(a):
            offsets = offs_t[:, 2 * a * COLS : 2 * (a + 1) * COLS]
            nc.vector.tensor_copy(xg[a][:], xw[:].bitcast(U32).indirect(offsets))
            nc.vector.tensor_copy(xgs[a][:], xs[:].indirect(offsets))

        def regroup_w1(a, on_scalar):
            for i in range(2):
                if on_scalar:
                    nc.scalar.copy(
                        w1g[a][:, i].rearrange("p t m -> p m t"),
                        w1w[a][:, i, :].bitcast(U32).rearrange("p (m t) -> p m t", t=PACK),
                    )
                else:
                    nc.vector.tensor_copy(
                        w1g[a][:, i].bitcast(I32).rearrange("p t m -> p m t"),
                        w1w[a][:, i, :].rearrange("p (m t) -> p m t", t=PACK),
                    )

        def text_hidden(a, offset):
            hidden = held([P, 2 * C, PACK], BF16, "hidden_t%d" % a, offset)
            for i in range(2):
                e = 2 * a + i
                slots = slice(i * C, (i + 1) * C)
                acc = bank_tile([P, H], "acc_t%d" % e, 6 * a + i)
                for t in range(PACK):
                    nc.tensor.matmul_mx(
                        out=acc[:, t * P : (t + 1) * P], lhsT=w1g[a][:, i, t, :].bitcast(FP8X4),
                        lhsT_scale=w1gs[4 * e :, t, :], rhs=xg[a][:, slots].bitcast(FP8X4),
                        rhs_scale=xgs[a][:, slots], start=True, stop=True,
                    )
                nc.scalar.activation(hidden[:, slots, :], acc[:].rearrange("p (t c) -> p c t", t=PACK), RELU)
            return hidden

        def text_rows(e, turn, offset, on_scalar):
            a, i = divmod(e, 2)
            slots = slice(i * C, (i + 1) * C)
            acc = bank_tile([P, H], "acc_t%d" % e, 6 + i)
            nc.tensor.matmul_mx(
                out=acc[:], lhsT=xg[a][:, slots].bitcast(FP8X4), lhsT_scale=xgs[a][:, slots],
                rhs=w1w[a][:, i, :].bitcast(FP8X4), rhs_scale=w1s[4 * e :, :], start=True, stop=True,
            )
            rows = held([P, H], BF16, "rows%d" % e, offset)
            if on_scalar:
                nc.scalar.activation(rows[:], acc[:], RELU)
            else:
                nc.vector.tensor_scalar_max(rows[:], acc[:], 0.0)
            pairs = rows[:].bitcast(F32)
            for u in range(2):
                nc.tensor.transpose(turn[:, i, u, :], pairs[:, u : H // 2 : 2], ident[:])

        def leave_turned(a, turn):
            hidden = held([P, 2 * C, PACK], BF16, "hidden_t%d" % a)
            nc.vector.tensor_copy(
                hidden[:].rearrange("p c t -> p (c t)").bitcast(F32).rearrange("p (i c u) -> p i c u", i=2, u=2),
                turn[:].rearrange("p i u c -> p i c u"),
            )
            return hidden

        def patch_hidden(e, offset=None):
            slots = slice(e * C, (e + 1) * C)
            acc = bank_tile([P, H], "acc_p%d" % e, e % 2)
            for s in range(Z_PASSES):
                w, ws = quantised[Z_PASSES * e + s]
                for t in range(PACK):
                    cols = slice(t * P, (t + 1) * P)
                    nc.tensor.matmul_mx(
                        out=acc[:, cols], lhsT=w[:, cols].bitcast(FP8X4), lhsT_scale=ws[:, cols],
                        rhs=zg[s][:, slots].bitcast(FP8X4), rhs_scale=zgs[4 * s :, slots],
                        start=(s == 0 and t == 0), stop=(s == Z_PASSES - 1 and t == PACK - 1),
                    )
            hidden = held([P, C, PACK], BF16, "hidden_p%d" % e, offset)
            nc.scalar.activation(hidden[:], acc[:].rearrange("p (t c) -> p c t", t=PACK), RELU)
            return hidden

        def quantise_hidden(hidden, name, offset=None):
            width = hidden.shape[1]
            codes = held([P, width], U32, "hcodes" + name, offset)
            scales = held([P, width], U8, "hscales" + name)
            nc.vector.quantize_mx(
                out=codes[:].bitcast(FP8X4), scales=scales[:], in_=hidden[:].rearrange("p c t -> p (c t)")
            )
            return codes, scales

        def second_product(operand, e0, count, name, first_bank):
            codes, scales = operand
            width = count * C
            per_bank = N_TILES // count
            banks = []
            for bank in range(count):
                acc = bank_tile([P, per_bank, width], "sums%s%d" % (name, bank), first_bank + bank)
                for i in range(count):
                    e = e0 + i
                    slots = slice(i * C, (i + 1) * C)
                    for b in range(per_bank):
                        cols = slice((bank * per_bank + b) * P, (bank * per_bank + b + 1) * P)
                        nc.tensor.matmul_mx(
                            out=acc[:, b, slots], lhsT=w2_of[e][:, cols].bitcast(FP8X4),
                            lhsT_scale=w2s[4 * e :, cols], rhs=codes[:, slots].bitcast(FP8X4),
                            rhs_scale=scales[:, slots], start=True, stop=True,
                        )
                banks.append(acc)
            return banks

        def block_sums(operand, e0, blocks, name, bank):
            codes, scales = operand
            width = codes.shape[1]
            acc = bank_tile([P, len(blocks), width], "sums" + name, bank)
            for i in range(width // C):
                slots = slice(i * C, (i + 1) * C)
                for n, b in enumerate(blocks):
                    cols = slice(b * P, (b + 1) * P)
                    nc.tensor.matmul_mx(
                        out=acc[:, n, slots], lhsT=w2_of[e0 + i][:, cols].bitcast(FP8X4),
                        lhsT_scale=w2s[4 * (e0 + i) :, cols], rhs=codes[:, slots].bitcast(FP8X4),
                        rhs_scale=scales[:, slots], start=True, stop=True,
                    )
            return acc

        def gated(bank, b0, b1, gate, name, offset=None, res=None):
            shape = [P, b1 - b0, bank.shape[2]]
            if res is None:
                tile = held(shape, F32, "res%s%d" % (name, b0), offset)
                res = tile[:]
            nc.vector.tensor_tensor(res, bank[:, b0:b1, :], gate.unsqueeze(1).to_broadcast(shape), MULT)
            return {b: res[:, b - b0, :] for b in range(b0, b1)}

        def gated_text(a, banks, b0, b1, offset=None, res=None):
            i = b0 // 2
            res = gated(banks[i], b0 - 2 * i, b1 - 2 * i, g1[a][:], "t%d%d" % (a, i), offset, res)
            return {2 * i + b: v for b, v in res.items()}

        def gated_patches(e, bank, b0, b1, offset=None, res=None):
            return gated(bank, b0, b1, g2[:, e * C : (e + 1) * C], "p%d" % e, offset, res)

        def scatter(window, offsets, values, on_scalar):
            if on_scalar:
                nc.scalar.activation(window[:].indirect(offsets), values, COPY)
            else:
                nc.vector.tensor_copy(window[:].indirect(offsets), values)

        def put_text(a, res, blocks, on_scalar=True):
            for b in blocks:
                scatter(text_out[b], offs_t[:, 2 * a * COLS : 2 * (a + 1) * COLS], res[b], on_scalar)

        def put_text_part(a, res, b, c0, c1, on_scalar):
            first = 2 * a * COLS
            scatter(text_out[b], offs_t[:, first + c0 : first + c1], res[b][:, 16 * c0 : 16 * c1], on_scalar)

        def put_patches(e, res, blocks, on_scalar=True):
            for b in blocks:
                scatter(patch_out[b], offs2_t[:, e * COLS : (e + 1) * COLS], res[b], on_scalar)

        grouped, quantised = {}, {}

        def cast_wz(k, on_scalar=0, halves=False):
            grouped[k] = held([P, PACK, P, PACK], BF16, "grouped%d" % k, grouped_at(k))
            dst = grouped[k][:].rearrange("p t m j -> p m j t")
            src = raw[k][:].rearrange("p j (m t) -> p m j t", t=PACK)
            if on_scalar:
                nc.scalar.copy(dst[:, P - on_scalar :], src[:, P - on_scalar :])
            cuts = (0, (P - on_scalar) // 2, P - on_scalar) if halves else (0, P - on_scalar)
            for m0, m1 in zip(cuts, cuts[1:]):
                nc.vector.tensor_copy(dst[:, m0:m1], src[:, m0:m1])

        def cast_last(k):
            grouped[k] = held([P, PACK, P, PACK], BF16, "grouped%d" % k, grouped_at(k))
            dst = grouped[k][:].rearrange("p t m j -> p m j t")
            src = raw[k][:].rearrange("p j (m t) -> p m j t", t=PACK)
            for t in (0, 2):
                nc.vector.tensor_copy(dst[:, :, :, t : t + 2], src[:, :, :, t : t + 2])

        def quantise_wz(k, parts=1):
            codes = held([P, H], U32, "wcodes%d" % k, grouped_at(PASSES) if k == PASSES - 1 else None)
            scales = held([P, H], U8, "wscales%d" % k)
            width = H // parts
            values = grouped[k][:].rearrange("p t m j -> p (t m j)")
            for c in range(0, H, width):
                nc.vector.quantize_mx(
                    out=codes[:, c : c + width].bitcast(FP8X4), scales=scales[:, c : c + width],
                    in_=values[:, PACK * c : PACK * (c + width)],
                )
            quantised[k] = codes, scales

        def store_text(b):
            nc.sync.dma_start(out=out[b * P : (b + 1) * P, 0:T], in_=text_out[b][:])

        def store_patches(b):
            nc.sync.dma_start(out=out[b * P : (b + 1) * P, T : T + Q], in_=patch_out[b][:])

        gather_text(0)
        regroup_w1(0, True)
        nc.vector.tensor_copy(w1gs[:].rearrange("p t m -> p m t"), w1s[:].rearrange("p (m t) -> p m t", t=PACK))
        gather_text(1)
        hidden = text_hidden(0, None)
        spread_gate2()
        for s in range(Z_PASSES):
            nc.vector.tensor_copy(zg[s][:], zw[s][:].bitcast(U32).indirect(offs2_t[:]))
        codes = quantise_hidden(hidden, "t0", grouped_at(0))
        for b in range(2):
            put_text(0, {b: gated(block_sums(codes, 0, (b,), "t0%d" % b, 2 + b), 0, 1, g1[0][:], "t0%d" % b)[0]}, (b,))
        res = gated(block_sums(codes, 0, (2, 3), "t02", 4), 0, 2, g1[0][:], "t02")
        first_sums = {2: res[0], 3: res[1]}
        put_text(0, first_sums, (2, 3))
        cast_last(0)
        nc.vector.tensor_copy(zgs[:], zs[:].indirect(offs2_t[:]))
        quantise_wz(0, 2)
        cast_last(1)
        quantise_wz(1, 2)
        hidden = patch_hidden(0)
        sums = {}
        for e in range(1, E):
            k = Z_PASSES * e
            if e == 1:
                cast_last(k)
                quantise_wz(k, 2)
            else:
                cast_wz(k, 0, True)
                put_patches(e - 2, gated_patches(e - 2, sums[e - 2], 2, 4, None, raw[k][:, 0:2, 0:C]), (2, 3))
                quantise_wz(k)
            codes = quantise_hidden(hidden, "p%d" % (e - 1), grouped_at(k) if e == 1 else None)
            sums[e - 1] = second_product(codes, e - 1, 1, "p%d" % (e - 1), 4 + (e - 1) % 2)[0]
            if e < E - 1:
                cast_wz(k + 1, P // 2 if e == 1 else 0, True)
            else:
                cast_last(k + 1)
            count = 2 if e < E - 1 else 1
            lead = raw[k + 1][:, 0:count, 0:C] if e < E - 1 else None
            put_patches(e - 1, gated_patches(e - 1, sums[e - 1], 0, count, None, lead), range(count))
            quantise_wz(k + 1, 1 if e < E - 1 else 2)
            hidden = patch_hidden(e)
        turn = bank_tile([P, 2, 2, C], "turn", 0)
        text_rows(2, turn, raw_at(PASSES - 1), False)
        text_rows(3, turn, grouped_at(PASSES) + 2 * C * 4, True)
        rest = gated_patches(2, sums[2], 1, 3, grouped_at(PASSES))
        put_patches(2, rest, (1,))
        codes = quantise_hidden(hidden, "p3")
        lead = block_sums(codes, 3, (0,), "p3a", 1)
        last = block_sums(codes, 3, (1, 2, 3), "p3b", 5)
        put_patches(2, rest, (2,), False)
        put_patches(3, gated_patches(3, lead, 0, 1), (0,))
        put_patches(3, {b + 1: v for b, v in gated(last, 0, 2, g2[:, 3 * C :], "p3b").items()}, (1, 2))
        hidden = leave_turned(1, turn)
        res = {3: gated(last, 2, 3, g2[:, 3 * C :], "p3b", grouped_at(PASSES) + 2 * C * 4)[2]}
        banks = second_product(quantise_hidden(hidden, "t1", grouped_at(1)), 2, 2, "t1", 2)
        put_patches(3, res, (3,), False)
        put_text(1, gated_text(1, banks, 0, 2), (0, 1))
        rest = gated_patches(2, sums[2], 3, 4, grouped_at(1))
        late = gated_text(1, banks, 2, 4)
        put_patches(2, rest, (3,), False)
        put_text_part(1, late, 2, COLS, 2 * COLS, False)
        put_text(1, late, (3,), False)
        put_text_part(1, late, 2, 0, COLS, True)
        for b in (0, 1, 2, 3):
            store_patches(b)
        for b in (0, 1, 3, 2):
            store_text(b)
